import numpy as np
import ml_dtypes


def mxq(x, axis, fmt="e4m3"):
    dtype, down = {"e4m3": (ml_dtypes.float8_e4m3fn, 7), "e5m2": (ml_dtypes.float8_e5m2, 14)}[fmt]
    v = np.moveaxis(np.asarray(x, np.float32).astype(ml_dtypes.bfloat16).astype(np.float64), axis, -1)
    blocks = v.reshape(v.shape[:-1] + (-1, 32))
    amax = np.abs(blocks).max(-1, keepdims=True)
    byte = np.maximum(np.where(amax > 0, np.frexp(amax)[1] - 1 + 127, 0) - down, 1)
    scale = np.exp2(byte - 127.0)
    codes = (blocks / scale).astype(np.float32).astype(dtype).astype(np.float64)
    return np.moveaxis((codes * scale).reshape(v.shape), -1, axis)


WIDE = False


def mx_kscale(k):
    if not WIDE:
        return np.ones(k)
    levels = np.array([10, -10, 5, -5, 0])
    if k % 512:
        return np.exp2(np.random.permutation(np.resize(levels, k // 32))).repeat(32)
    a = np.empty((k // 512, 16))
    for p in range(k // 512):
        a[p, :8] = np.random.permutation(np.resize(levels, 8))
        for g in range(8):
            far = levels[np.abs(levels - a[p, g]) >= 10]
            a[p, g + 8] = far[np.random.randint(len(far))]
    return np.exp2(a.ravel()).repeat(32)


def f64(x):
    return np.asarray(x).astype(np.float64)


def striped(idx):
    return np.tile(idx.reshape(-1, 16).T, (8, 1)).astype(np.uint16)


def unstriped(offs):
    return offs[:16].T.reshape(-1).astype(np.int64)


def pack_weight(w):
    k, n = w.shape
    w = f64(np.asarray(w, np.float32).astype(ml_dtypes.bfloat16)).reshape(k // 32, 32, n)
    amax = np.abs(w).max(1)
    byte = np.clip(np.where(amax > 0, np.frexp(amax)[1] - 1 + 127 - 7, 1), 1, 254)
    scaled = (w * np.exp2(127.0 - byte)[:, None, :]).reshape(k, n).astype(np.float32)
    words = np.ascontiguousarray(scaled.reshape(k // 512, 128, 4, n).transpose(0, 1, 3, 2)).astype(ml_dtypes.float8_e4m3fn).view(np.uint8)
    return words, np.ascontiguousarray(byte.astype(np.uint8).reshape(k // 512, 16, n))


def unpack_weight(words, scales):
    g, p, n, _ = words.shape
    vals = np.ascontiguousarray(words).view(ml_dtypes.float8_e4m3fn).astype(np.float64) * np.repeat(np.exp2(scales.astype(np.float64) - 127.0), 8, axis=1)[..., None]
    return vals.transpose(0, 1, 3, 2).reshape(g * 512, n)


def relu(v):
    return np.maximum(v, 0.0)


K, T, D, S, V, N = 512, 1024, 6, 3072, 512, 128


def setup_inputs():
    n = np.random.standard_normal
    s = mx_kscale(K)[:, None]
    words, scales = pack_weight(n((K, N)) / np.sqrt(K) / s)
    return {
        "xT": (n((K, T)) * s).astype(np.float32),
        "w_words": words,
        "w_scales": scales,
        "b": (0.3 * n((N, 1))).astype(np.float32),
        "gate": np.tile(np.random.uniform(0.2, 1.0, (D, 1, V)) / np.sqrt(D), (1, N, 1)).astype(np.float32),
        "pos1": striped(np.random.permutation(T)[:V]),
        "pos2": striped(np.random.permutation(T)[:V]),
        "pos3": striped(np.random.permutation(T)[:V]),
        "pos4": striped(np.random.permutation(T)[:V]),
        "pos5": striped(np.random.permutation(T)[:V]),
        "pos6": striped(np.random.permutation(T)[:V]),
    }


def reference(xT, w_words, w_scales, b, gate, pos1, pos2, pos3, pos4, pos5, pos6):
    w = unpack_weight(w_words, w_scales)
    y = w.T @ mxq(f64(xT), 0, "e4m3")
    y = relu(y + f64(b))
    return sum(f64(gate[d]) * y[:, unstriped(p)] for d, p in enumerate((pos1, pos2, pos3, pos4, pos5, pos6)))

@@ -1,0 +1,160 @@
+from contextlib import ExitStack
+
+import concourse.mybir as mybir
+
+K, T, D, V, N = 512, 1024, 6, 512, 128
+P = 128
+PACK = 4
+FLOPS = 2 * K * N * T + 2 * D * N * V
+
+F32 = mybir.dt.float32
+BF16 = mybir.dt.bfloat16
+I32 = mybir.dt.int32
+U32 = mybir.dt.uint32
+U16 = mybir.dt.uint16
+U8 = mybir.dt.uint8
+FP8X4 = mybir.dt.float8_e4m3fn_x4
+RELU = mybir.ActivationFunctionType.Relu
+MULT = mybir.AluOpType.mult
+ADD = mybir.AluOpType.add
+
+LOADS = ((0, 512), (512, 832), (832, 1024))
+HALF = V // 2
+
+
+def tile_picked_agg_lin_relu_sub_l_kernel(
+    tc, xT, w_words, w_scales, b, gate, pos1, pos2, pos3, pos4, pos5, pos6, out
+):
+    nc = tc.nc
+    with ExitStack() as ctx:
+        lists = ctx.enter_context(tc.tile_pool(name="lists", bufs=1))
+        keep = ctx.enter_context(tc.tile_pool(name="keep", bufs=1))
+        psum = ctx.enter_context(tc.psum_pool(name="psum", bufs=1))
+
+        offsets = [lists.tile([P, V // 16], U16, name=f"offsets{d}") for d in range(D)]
+
+        w_plane = keep.tile([P, N], U8, align_bytes=64)
+        nc.vector.memset(w_plane[:].bitcast(I32), 0)
+        warm = keep.tile([P, 8], F32)
+        nc.vector.memset(warm[:], 0.0)
+
+        w_codes = keep.tile([P, N * PACK], U8, align_bytes=64)
+        nc.scalar.dma_start(out=w_codes[:].bitcast(I32), in_=w_words.rearrange("a p m r -> (a p) (m r)").bitcast(I32))
+        bias = keep.tile([P, 1], F32)
+        nc.scalar.dma_start(out=bias[:], in_=b)
+        scale_rows = w_scales.rearrange("a q m -> (a q) m")
+        for q in range(4):
+            nc.scalar.dma_start(
+                out=w_plane[32 * q : 32 * q + 4, :].bitcast(I32), in_=scale_rows[4 * q : 4 * q + 4, :].bitcast(I32)
+            )
+        warm_out = keep.tile([P, 8], F32)
+        nc.scalar.activation(warm_out[:], warm[:], RELU)
+
+        x_rows = xT.rearrange("(p j) t -> p j t", j=PACK)
+        raws = []
+        for c, (t0, t1) in enumerate(LOADS):
+            raw = keep.tile([P, PACK, t1 - t0], F32, name=f"raw{c}")
+            nc.sync.dma_start(out=raw[:], in_=x_rows[:, :, t0:t1])
+            raws.append(raw)
+
+        gates = [keep.tile([P, d1 - d0, V], F32, name=f"gates{d0}") for d0, d1 in ((0, 1), (1, 3), (3, 6))]
+        positions = (pos1, pos2, pos3, pos4, pos5, pos6)
+
+        def load_list(d):
+            nc.sync.dma_start(out=offsets[d][:], in_=positions[d])
+
+        def load_gates(g, d0, d1):
+            nc.sync.dma_start(out=gates[g][:], in_=gate[d0:d1].rearrange("d p v -> p d v"))
+
+        load_list(0)
+        load_gates(0, 0, 1)
+        load_list(1)
+        load_list(2)
+        load_gates(1, 1, 3)
+        load_list(3)
+        load_list(4)
+        load_list(5)
+        load_gates(2, 3, 6)
+
+        grouped = keep.tile([P, T, PACK], BF16, align_bytes=64)
+        codes = keep.tile([P, T], U32, align_bytes=64)
+        planes = keep.tile([P, T], U8, align_bytes=64)
+        y = keep.tile([P, T], F32)
+        banks = {}
+
+        def loaded(t0, t1):
+            for raw, (l0, l1) in zip(raws, LOADS):
+                if l0 <= t0 and t1 <= l1:
+                    return raw[:, :, t0 - l0 : t1 - l0].rearrange("p j t -> p t j")
+
+        def by_vector(t0, t1):
+            nc.vector.tensor_copy(grouped[:, t0:t1, :], loaded(t0, t1))
+
+        def by_scalar(t0, t1):
+            nc.scalar.copy(grouped[:, t0:t1, :], loaded(t0, t1))
+
+        def project(t0, t1):
+            nc.vector.quantize_mx(
+                out=codes[:, t0:t1].bitcast(FP8X4),
+                scales=planes[:, t0:t1],
+                in_=grouped[:, t0:t1, :].rearrange("p t j -> p (t j)"),
+            )
+            acc = psum.tile([P, t1 - t0], F32, name=f"acc{t0}")
+            nc.tensor.matmul_mx(
+                out=acc[:],
+                lhsT=w_codes[:].bitcast(FP8X4),
+                lhsT_scale=w_plane[:],
+                rhs=codes[:, t0:t1].bitcast(FP8X4),
+                rhs_scale=planes[:, t0:t1],
+                start=True,
+                stop=True,
+            )
+            banks[t0] = acc
+
+        def finish(t0, t1):
+            nc.scalar.activation(y[:, t0:t1], banks[t0][:], RELU, bias=bias[:])
+
+        by_vector(0, 304)
+        by_scalar(304, 512)
+        project(0, 256)
+        project(256, 512)
+        by_vector(512, 704)
+        by_scalar(704, 768)
+        finish(0, 256)
+        by_vector(768, 832)
+        project(512, 768)
+        finish(256, 512)
+        by_vector(832, 912)
+        by_scalar(912, 1024)
+        project(768, 896)
+        project(896, 1024)
+        finish(512, 768)
+        finish(768, 896)
+        finish(896, 1024)
+
+        gate_of = [gates[0][:, 0, :], gates[1][:, 0, :], gates[1][:, 1, :]] + [gates[2][:, d, :] for d in range(3)]
+        terms = [keep.tile([P, V], F32, name=f"term{d}") for d in range(D)]
+        sums = [keep.tile([P, V], F32, name=f"sum{d}") for d in range(5)]
+
+        def neighbour(d, v0=0, v1=V):
+            idx = offsets[d][:, v0 // 16 : v1 // 16]
+            nc.vector.tensor_tensor(terms[d][:, v0:v1], y[:].indirect(idx), gate_of[d][:, v0:v1], MULT)
+
+        def add(dst, a, b_, v0=0, v1=V):
+            nc.vector.tensor_tensor(dst[:, v0:v1], a[:, v0:v1], b_[:, v0:v1], ADD)
+
+        neighbour(0)
+        neighbour(1)
+        neighbour(2)
+        add(sums[0], terms[0], terms[1])
+        neighbour(3)
+        add(sums[1], sums[0], terms[2])
+        neighbour(4)
+        add(sums[2], sums[1], terms[3])
+        neighbour(5, 0, HALF)
+        add(sums[3], sums[2], terms[4])
+        neighbour(5, HALF, V)
+        add(sums[4], sums[3], terms[5], 0, HALF)
+        nc.sync.dma_start(out=out[:, 0:HALF], in_=sums[4][:, 0:HALF])
+        add(sums[4], sums[3], terms[5], HALF, V)
+        nc.sync.dma_start(out=out[:, HALF:V], in_=sums[4][:, HALF:V])

@@ -1,6 +1,7 @@
 from contextlib import ExitStack
 
 import concourse.mybir as mybir
+from concourse.masks import make_identity
 
 K, T, D, V, N = 512, 1024, 6, 512, 128
 P = 128
@@ -32,6 +33,9 @@ def tile_picked_agg_lin_relu_sub_l_kernel(
         psum = ctx.enter_context(tc.psum_pool(name="psum", bufs=1))
 
         offsets = [lists.tile([P, V // 16], U16, name=f"offsets{d}") for d in range(D)]
+
+        ident = keep.tile([P, P], F32)
+        make_identity(nc, ident[:])
 
         w_plane = keep.tile([P, N], U8, align_bytes=64)
         nc.vector.memset(w_plane[:].bitcast(I32), 0)
@@ -85,13 +89,16 @@ def tile_picked_agg_lin_relu_sub_l_kernel(
         def loaded(t0, t1):
             for raw, (l0, l1) in zip(raws, LOADS):
                 if l0 <= t0 and t1 <= l1:
-                    return raw[:, :, t0 - l0 : t1 - l0].rearrange("p j t -> p t j")
+                    return raw[:, :, t0 - l0 : t1 - l0].rearrange("p j (c i) -> p c j i", i=PACK)
+
+        def laid(t0, t1):
+            return grouped[:, t0:t1, :].rearrange("p (c i) j -> p c j i", i=PACK)
 
         def by_vector(t0, t1):
-            nc.vector.tensor_copy(grouped[:, t0:t1, :], loaded(t0, t1))
+            nc.vector.tensor_copy(laid(t0, t1), loaded(t0, t1))
 
         def by_scalar(t0, t1):
-            nc.scalar.copy(grouped[:, t0:t1, :], loaded(t0, t1))
+            nc.scalar.copy(laid(t0, t1), loaded(t0, t1))
 
         def project(t0, t1):
             nc.vector.quantize_mx(
@@ -99,9 +106,9 @@ def tile_picked_agg_lin_relu_sub_l_kernel(
                 scales=planes[:, t0:t1],
                 in_=grouped[:, t0:t1, :].rearrange("p t j -> p (t j)"),
             )
-            acc = psum.tile([P, t1 - t0], F32, name=f"acc{t0}")
+            acc = psum.tile([P, V], F32, name=f"bank{len(banks)}")
             nc.tensor.matmul_mx(
-                out=acc[:],
+                out=acc[:, 0 : t1 - t0],
                 lhsT=w_codes[:].bitcast(FP8X4),
                 lhsT_scale=w_plane[:],
                 rhs=codes[:, t0:t1].bitcast(FP8X4),
@@ -112,7 +119,7 @@ def tile_picked_agg_lin_relu_sub_l_kernel(
             banks[t0] = acc
 
         def finish(t0, t1):
-            nc.scalar.activation(y[:, t0:t1], banks[t0][:], RELU, bias=bias[:])
+            nc.scalar.activation(y[:, t0:t1], banks[t0][:, 0 : t1 - t0], RELU, bias=bias[:])
 
         by_vector(0, 304)
         by_scalar(304, 512)
@@ -134,27 +141,43 @@ def tile_picked_agg_lin_relu_sub_l_kernel(
 
         gate_of = [gates[0][:, 0, :], gates[1][:, 0, :], gates[1][:, 1, :]] + [gates[2][:, d, :] for d in range(3)]
         terms = [keep.tile([P, V], F32, name=f"term{d}") for d in range(D)]
-        sums = [keep.tile([P, V], F32, name=f"sum{d}") for d in range(5)]
+        blocks = V // P
+        turned = [psum.tile([P, V], F32, name=f"bank{(5 + c) % 8}") for c in range(blocks)]
+        back = [psum.tile([P, V], F32, name=f"bank{1 + h}") for h in range(2)]
+        partial = [keep.tile([P, P], F32, name=f"partial{c}") for c in range(blocks)]
+        result = [keep.tile([P, HALF], F32, name=f"result{h}") for h in range(2)]
 
         def neighbour(d, v0=0, v1=V):
             idx = offsets[d][:, v0 // 16 : v1 // 16]
             nc.vector.tensor_tensor(terms[d][:, v0:v1], y[:].indirect(idx), gate_of[d][:, v0:v1], MULT)
 
-        def add(dst, a, b_, v0=0, v1=V):
-            nc.vector.tensor_tensor(dst[:, v0:v1], a[:, v0:v1], b_[:, v0:v1], ADD)
+        def accumulate(d, c):
+            nc.tensor.matmul(
+                turned[c][:, 0:P],
+                lhsT=terms[d][:, c * P : (c + 1) * P],
+                rhs=ident[:],
+                is_transpose=True,
+                start=(d == 0),
+                stop=(d == D - 2),
+            )
 
-        neighbour(0)
-        neighbour(1)
-        neighbour(2)
-        add(sums[0], terms[0], terms[1])
-        neighbour(3)
-        add(sums[1], sums[0], terms[2])
-        neighbour(4)
-        add(sums[2], sums[1], terms[3])
-        neighbour(5, 0, HALF)
-        add(sums[3], sums[2], terms[4])
-        neighbour(5, HALF, V)
-        add(sums[4], sums[3], terms[5], 0, HALF)
-        nc.sync.dma_start(out=out[:, 0:HALF], in_=sums[4][:, 0:HALF])
-        add(sums[4], sums[3], terms[5], HALF, V)
-        nc.sync.dma_start(out=out[:, HALF:V], in_=sums[4][:, HALF:V])
+        def turn_back(c):
+            nc.scalar.copy(partial[c][:], turned[c][:, 0:P])
+            nc.tensor.transpose(back[c // 2][:, (c % 2) * P : (c % 2 + 1) * P], partial[c][:], ident[:])
+
+        for d in range(D - 2):
+            neighbour(d)
+            for c in range(blocks):
+                accumulate(d, c)
+        for h in range(2):
+            neighbour(D - 2, h * HALF, (h + 1) * HALF)
+            for c in (2 * h, 2 * h + 1):
+                accumulate(D - 2, c)
+            for c in (2 * h, 2 * h + 1):
+                turn_back(c)
+        for h in range(2):
+            neighbour(D - 1, h * HALF, (h + 1) * HALF)
+        for h in range(2):
+            cols = slice(h * HALF, (h + 1) * HALF)
+            nc.vector.tensor_tensor(result[h][:], back[h][:, 0:HALF], terms[D - 1][:, cols], ADD)
+            nc.sync.dma_start(out=out[:, cols], in_=result[h][:])

@@ -18,6 +18,7 @@ FP8X4 = mybir.dt.float8_e4m3fn_x4
 RELU = mybir.ActivationFunctionType.Relu
 MULT = mybir.AluOpType.mult
 ADD = mybir.AluOpType.add
+MAX = mybir.AluOpType.max
 
 LOADS = ((0, 512), (512, 832), (832, 1024))
 HALF = V // 2
@@ -45,12 +46,6 @@ def tile_picked_agg_lin_relu_sub_l_kernel(
         w_codes = keep.tile([P, N * PACK], U8, align_bytes=64)
         nc.scalar.dma_start(out=w_codes[:].bitcast(I32), in_=w_words.rearrange("a p m r -> (a p) (m r)").bitcast(I32))
         bias = keep.tile([P, 1], F32)
-        nc.scalar.dma_start(out=bias[:], in_=b)
-        scale_rows = w_scales.rearrange("a q m -> (a q) m")
-        for q in range(4):
-            nc.scalar.dma_start(
-                out=w_plane[32 * q : 32 * q + 4, :].bitcast(I32), in_=scale_rows[4 * q : 4 * q + 4, :].bitcast(I32)
-            )
         warm_out = keep.tile([P, 8], F32)
         nc.scalar.activation(warm_out[:], warm[:], RELU)
 
@@ -60,6 +55,15 @@ def tile_picked_agg_lin_relu_sub_l_kernel(
             raw = keep.tile([P, PACK, t1 - t0], F32, name=f"raw{c}")
             nc.sync.dma_start(out=raw[:], in_=x_rows[:, :, t0:t1])
             raws.append(raw)
+            if c == 2:
+                nc.sync.dma_start(out=bias[:], in_=b)
+            if c == 0:
+                scale_rows = w_scales.rearrange("a q m -> (a q) m")
+                for q in range(4):
+                    nc.sync.dma_start(
+                        out=w_plane[32 * q : 32 * q + 4, :].bitcast(I32),
+                        in_=scale_rows[4 * q : 4 * q + 4, :].bitcast(I32),
+                    )
 
         gates = [keep.tile([P, d1 - d0, V], F32, name=f"gates{d0}") for d0, d1 in ((0, 1), (1, 3), (3, 6))]
         positions = (pos1, pos2, pos3, pos4, pos5, pos6)
@@ -100,15 +104,16 @@ def tile_picked_agg_lin_relu_sub_l_kernel(
         def by_scalar(t0, t1):
             nc.scalar.copy(laid(t0, t1), loaded(t0, t1))
 
-        def project(t0, t1):
+        def project(t0, t1, home):
             nc.vector.quantize_mx(
                 out=codes[:, t0:t1].bitcast(FP8X4),
                 scales=planes[:, t0:t1],
                 in_=grouped[:, t0:t1, :].rearrange("p t j -> p (t j)"),
             )
-            acc = psum.tile([P, V], F32, name=f"bank{len(banks)}")
+            if home not in banks:
+                banks[home] = psum.tile([P, V], F32, name=f"bank{len(banks)}")
             nc.tensor.matmul_mx(
-                out=acc[:, 0 : t1 - t0],
+                out=banks[home][:, t0 - home : t1 - home],
                 lhsT=w_codes[:].bitcast(FP8X4),
                 lhsT_scale=w_plane[:],
                 rhs=codes[:, t0:t1].bitcast(FP8X4),
@@ -116,27 +121,29 @@ def tile_picked_agg_lin_relu_sub_l_kernel(
                 start=True,
                 stop=True,
             )
-            banks[t0] = acc
 
         def finish(t0, t1):
             nc.scalar.activation(y[:, t0:t1], banks[t0][:, 0 : t1 - t0], RELU, bias=bias[:])
 
+        def finish_on_vector(t0, t1):
+            nc.vector.tensor_scalar(y[:, t0:t1], banks[t0][:, 0 : t1 - t0], bias[:], 0.0, ADD, MAX)
+
         by_vector(0, 304)
         by_scalar(304, 512)
-        project(0, 256)
-        project(256, 512)
-        by_vector(512, 704)
-        by_scalar(704, 768)
-        finish(0, 256)
-        by_vector(768, 832)
-        project(512, 768)
-        finish(256, 512)
-        by_vector(832, 912)
-        by_scalar(912, 1024)
-        project(768, 896)
-        project(896, 1024)
+        project(0, 256, 0)
+        project(256, 512, 0)
+        by_vector(512, 640)
+        by_vector(640, 704)
+        by_scalar(704, 832)
+        project(512, 768, 512)
+        by_vector(832, 896)
+        by_vector(896, 960)
+        by_scalar(960, 1024)
+        project(768, 896, 768)
+        project(896, 1024, 896)
+        finish(0, 512)
         finish(512, 768)
-        finish(768, 896)
+        finish_on_vector(768, 896)
         finish(896, 1024)
 
         gate_of = [gates[0][:, 0, :], gates[1][:, 0, :], gates[1][:, 1, :]] + [gates[2][:, d, :] for d in range(3)]
@@ -169,11 +176,11 @@ def tile_picked_agg_lin_relu_sub_l_kernel(
             neighbour(d)
             for c in range(blocks):
                 accumulate(d, c)
-        for h in range(2):
-            neighbour(D - 2, h * HALF, (h + 1) * HALF)
-            for c in (2 * h, 2 * h + 1):
+        for c0, c1 in ((0, 2), (2, 3), (3, 4)):
+            neighbour(D - 2, c0 * P, c1 * P)
+            for c in range(c0, c1):
                 accumulate(D - 2, c)
-            for c in (2 * h, 2 * h + 1):
+            for c in range(c0, c1):
                 turn_back(c)
         for h in range(2):
             neighbour(D - 1, h * HALF, (h + 1) * HALF)

@@ -65,24 +65,10 @@ def tile_picked_agg_lin_relu_sub_l_kernel(
                         in_=scale_rows[4 * q : 4 * q + 4, :].bitcast(I32),
                     )
 
-        gates = [keep.tile([P, d1 - d0, V], F32, name=f"gates{d0}") for d0, d1 in ((0, 1), (1, 3), (3, 6))]
-        positions = (pos1, pos2, pos3, pos4, pos5, pos6)
-
-        def load_list(d):
-            nc.sync.dma_start(out=offsets[d][:], in_=positions[d])
-
-        def load_gates(g, d0, d1):
-            nc.sync.dma_start(out=gates[g][:], in_=gate[d0:d1].rearrange("d p v -> p d v"))
-
-        load_list(0)
-        load_gates(0, 0, 1)
-        load_list(1)
-        load_list(2)
-        load_gates(1, 1, 3)
-        load_list(3)
-        load_list(4)
-        load_list(5)
-        load_gates(2, 3, 6)
+        gates = [keep.tile([P, V], F32, name=f"gate{d}") for d in range(D)]
+        for d, pos in enumerate((pos1, pos2, pos3, pos4, pos5, pos6)):
+            nc.sync.dma_start(out=offsets[d][:], in_=pos)
+            nc.sync.dma_start(out=gates[d][:], in_=gate[d])
 
         grouped = keep.tile([P, T, PACK], BF16, align_bytes=64)
         codes = keep.tile([P, T], U32, align_bytes=64)
@@ -128,8 +114,9 @@ def tile_picked_agg_lin_relu_sub_l_kernel(
         def finish_on_vector(t0, t1):
             nc.vector.tensor_scalar(y[:, t0:t1], banks[t0][:, 0 : t1 - t0], bias[:], 0.0, ADD, MAX)
 
-        by_vector(0, 304)
-        by_scalar(304, 512)
+        by_vector(0, 256)
+        by_vector(256, 288)
+        by_scalar(288, 512)
         project(0, 256, 0)
         project(256, 512, 0)
         by_vector(512, 640)
@@ -137,8 +124,8 @@ def tile_picked_agg_lin_relu_sub_l_kernel(
         by_scalar(704, 832)
         project(512, 768, 512)
         by_vector(832, 896)
-        by_vector(896, 960)
-        by_scalar(960, 1024)
+        by_vector(896, 928)
+        by_scalar(928, 1024)
         project(768, 896, 768)
         project(896, 1024, 896)
         finish(0, 512)
@@ -146,17 +133,15 @@ def tile_picked_agg_lin_relu_sub_l_kernel(
         finish_on_vector(768, 896)
         finish(896, 1024)
 
-        gate_of = [gates[0][:, 0, :], gates[1][:, 0, :], gates[1][:, 1, :]] + [gates[2][:, d, :] for d in range(3)]
         terms = [keep.tile([P, V], F32, name=f"term{d}") for d in range(D)]
         blocks = V // P
         turned = [psum.tile([P, V], F32, name=f"bank{(5 + c) % 8}") for c in range(blocks)]
-        back = [psum.tile([P, V], F32, name=f"bank{1 + h}") for h in range(2)]
+        back = {c0: psum.tile([P, V], F32, name=f"bank{bank}") for c0, bank in ((0, 1), (2, 2), (3, 4))}
         partial = [keep.tile([P, P], F32, name=f"partial{c}") for c in range(blocks)]
-        result = [keep.tile([P, HALF], F32, name=f"result{h}") for h in range(2)]
 
         def neighbour(d, v0=0, v1=V):
             idx = offsets[d][:, v0 // 16 : v1 // 16]
-            nc.vector.tensor_tensor(terms[d][:, v0:v1], y[:].indirect(idx), gate_of[d][:, v0:v1], MULT)
+            nc.vector.tensor_tensor(terms[d][:, v0:v1], y[:].indirect(idx), gates[d][:, v0:v1], MULT)
 
         def accumulate(d, c):
             nc.tensor.matmul(
@@ -168,9 +153,9 @@ def tile_picked_agg_lin_relu_sub_l_kernel(
                 stop=(d == D - 2),
             )
 
-        def turn_back(c):
+        def turn_back(c0, c):
             nc.scalar.copy(partial[c][:], turned[c][:, 0:P])
-            nc.tensor.transpose(back[c // 2][:, (c % 2) * P : (c % 2 + 1) * P], partial[c][:], ident[:])
+            nc.tensor.transpose(back[c0][:, (c - c0) * P : (c - c0 + 1) * P], partial[c][:], ident[:])
 
         for d in range(D - 2):
             neighbour(d)
@@ -181,10 +166,12 @@ def tile_picked_agg_lin_relu_sub_l_kernel(
             for c in range(c0, c1):
                 accumulate(D - 2, c)
             for c in range(c0, c1):
-                turn_back(c)
+                turn_back(c0, c)
         for h in range(2):
             neighbour(D - 1, h * HALF, (h + 1) * HALF)
-        for h in range(2):
-            cols = slice(h * HALF, (h + 1) * HALF)
-            nc.vector.tensor_tensor(result[h][:], back[h][:, 0:HALF], terms[D - 1][:, cols], ADD)
-            nc.sync.dma_start(out=out[:, cols], in_=result[h][:])
+        for c0, c1 in ((0, 2), (2, 3), (3, 4)):
+            cols = slice(c0 * P, c1 * P)
+            result = keep.tile([P, (c1 - c0) * P], F32, name=f"result{c0}")
+            turned_back = back[c0][:, 0 : (c1 - c0) * P]
+            nc.vector.tensor_tensor(result[:], turned_back, terms[D - 1][:, cols], ADD)
+            nc.sync.dma_start(out=out[:, cols], in_=result[:])

@@ -6,6 +6,8 @@ from concourse.masks import make_identity
 K, T, D, V, N = 512, 1024, 6, 512, 128
 P = 128
 PACK = 4
+BANK = 512
+LINE = 4
 FLOPS = 2 * K * N * T + 2 * D * N * V
 
 F32 = mybir.dt.float32
@@ -21,6 +23,7 @@ ADD = mybir.AluOpType.add
 MAX = mybir.AluOpType.max
 
 LOADS = ((0, 512), (512, 832), (832, 1024))
+PIECES = ((0, 2), (2, 3), (3, 4))
 HALF = V // 2
 
 
@@ -33,37 +36,39 @@ def tile_picked_agg_lin_relu_sub_l_kernel(
         keep = ctx.enter_context(tc.tile_pool(name="keep", bufs=1))
         psum = ctx.enter_context(tc.psum_pool(name="psum", bufs=1))
 
+        def bank(n):
+            return psum.tile([P, BANK], F32, name=f"bank{n}")
+
         offsets = [lists.tile([P, V // 16], U16, name=f"offsets{d}") for d in range(D)]
 
         ident = keep.tile([P, P], F32)
         make_identity(nc, ident[:])
 
-        w_plane = keep.tile([P, N], U8, align_bytes=64)
-        nc.vector.memset(w_plane[:].bitcast(I32), 0)
-        warm = keep.tile([P, 8], F32)
-        nc.vector.memset(warm[:], 0.0)
+        w_scale = keep.tile([P, N], U8, align_bytes=64)
+        nc.vector.memset(w_scale[:].bitcast(I32), 0)
 
         w_codes = keep.tile([P, N * PACK], U8, align_bytes=64)
         nc.scalar.dma_start(out=w_codes[:].bitcast(I32), in_=w_words.rearrange("a p m r -> (a p) (m r)").bitcast(I32))
         bias = keep.tile([P, 1], F32)
-        warm_out = keep.tile([P, 8], F32)
-        nc.scalar.activation(warm_out[:], warm[:], RELU)
 
         x_rows = xT.rearrange("(p j) t -> p j t", j=PACK)
         raws = []
-        for c, (t0, t1) in enumerate(LOADS):
-            raw = keep.tile([P, PACK, t1 - t0], F32, name=f"raw{c}")
+
+        def load_x(t0, t1):
+            raw = keep.tile([P, PACK, t1 - t0], F32, name=f"raw{len(raws)}")
             nc.sync.dma_start(out=raw[:], in_=x_rows[:, :, t0:t1])
             raws.append(raw)
-            if c == 2:
-                nc.sync.dma_start(out=bias[:], in_=b)
-            if c == 0:
-                scale_rows = w_scales.rearrange("a q m -> (a q) m")
-                for q in range(4):
-                    nc.sync.dma_start(
-                        out=w_plane[32 * q : 32 * q + 4, :].bitcast(I32),
-                        in_=scale_rows[4 * q : 4 * q + 4, :].bitcast(I32),
-                    )
+
+        load_x(*LOADS[0])
+        scale_rows = w_scales.rearrange("a q m -> (a q) m")
+        for quadrant in range(4):
+            nc.sync.dma_start(
+                out=w_scale[32 * quadrant : 32 * quadrant + 4, :].bitcast(I32),
+                in_=scale_rows[4 * quadrant : 4 * quadrant + 4, :].bitcast(I32),
+            )
+        load_x(*LOADS[1])
+        load_x(*LOADS[2])
+        nc.sync.dma_start(out=bias[:], in_=b)
 
         gates = [keep.tile([P, V], F32, name=f"gate{d}") for d in range(D)]
         for d, pos in enumerate((pos1, pos2, pos3, pos4, pos5, pos6)):
@@ -71,77 +76,76 @@ def tile_picked_agg_lin_relu_sub_l_kernel(
             nc.sync.dma_start(out=gates[d][:], in_=gate[d])
 
         grouped = keep.tile([P, T, PACK], BF16, align_bytes=64)
-        codes = keep.tile([P, T], U32, align_bytes=64)
-        planes = keep.tile([P, T], U8, align_bytes=64)
+        x_codes = keep.tile([P, T], U32, align_bytes=64)
+        x_scale = keep.tile([P, T], U8, align_bytes=64)
         y = keep.tile([P, T], F32)
-        banks = {}
+        products = {}
 
         def loaded(t0, t1):
             for raw, (l0, l1) in zip(raws, LOADS):
                 if l0 <= t0 and t1 <= l1:
-                    return raw[:, :, t0 - l0 : t1 - l0].rearrange("p j (c i) -> p c j i", i=PACK)
+                    return raw[:, :, t0 - l0 : t1 - l0].rearrange("p j (c i) -> p c j i", i=LINE)
 
         def laid(t0, t1):
-            return grouped[:, t0:t1, :].rearrange("p (c i) j -> p c j i", i=PACK)
+            return grouped[:, t0:t1, :].rearrange("p (c i) j -> p c j i", i=LINE)
 
-        def by_vector(t0, t1):
+        def copy_on_vector(t0, t1):
             nc.vector.tensor_copy(laid(t0, t1), loaded(t0, t1))
 
-        def by_scalar(t0, t1):
+        def copy_on_scalar(t0, t1):
             nc.scalar.copy(laid(t0, t1), loaded(t0, t1))
 
-        def project(t0, t1, home):
+        def project(t0, t1, first):
             nc.vector.quantize_mx(
-                out=codes[:, t0:t1].bitcast(FP8X4),
-                scales=planes[:, t0:t1],
+                out=x_codes[:, t0:t1].bitcast(FP8X4),
+                scales=x_scale[:, t0:t1],
                 in_=grouped[:, t0:t1, :].rearrange("p t j -> p (t j)"),
             )
-            if home not in banks:
-                banks[home] = psum.tile([P, V], F32, name=f"bank{len(banks)}")
+            if first not in products:
+                products[first] = bank(len(products))
             nc.tensor.matmul_mx(
-                out=banks[home][:, t0 - home : t1 - home],
+                out=products[first][:, t0 - first : t1 - first],
                 lhsT=w_codes[:].bitcast(FP8X4),
-                lhsT_scale=w_plane[:],
-                rhs=codes[:, t0:t1].bitcast(FP8X4),
-                rhs_scale=planes[:, t0:t1],
+                lhsT_scale=w_scale[:],
+                rhs=x_codes[:, t0:t1].bitcast(FP8X4),
+                rhs_scale=x_scale[:, t0:t1],
                 start=True,
                 stop=True,
             )
 
-        def finish(t0, t1):
-            nc.scalar.activation(y[:, t0:t1], banks[t0][:, 0 : t1 - t0], RELU, bias=bias[:])
+        def relu_on_scalar(t0, t1):
+            nc.scalar.activation(y[:, t0:t1], products[t0][:, 0 : t1 - t0], RELU, bias=bias[:])
 
-        def finish_on_vector(t0, t1):
-            nc.vector.tensor_scalar(y[:, t0:t1], banks[t0][:, 0 : t1 - t0], bias[:], 0.0, ADD, MAX)
+        def relu_on_vector(t0, t1):
+            nc.vector.tensor_scalar(y[:, t0:t1], products[t0][:, 0 : t1 - t0], bias[:], 0.0, ADD, MAX)
 
-        by_vector(0, 256)
-        by_vector(256, 288)
-        by_scalar(288, 512)
+        copy_on_vector(0, 256)
+        copy_on_vector(256, 288)
+        copy_on_scalar(288, 512)
         project(0, 256, 0)
         project(256, 512, 0)
-        by_vector(512, 640)
-        by_vector(640, 704)
-        by_scalar(704, 832)
+        copy_on_vector(512, 704)
+        copy_on_scalar(704, 832)
         project(512, 768, 512)
-        by_vector(832, 896)
-        by_vector(896, 928)
-        by_scalar(928, 1024)
+        copy_on_vector(832, 896)
+        copy_on_vector(896, 928)
+        copy_on_scalar(928, 1024)
         project(768, 896, 768)
         project(896, 1024, 896)
-        finish(0, 512)
-        finish(512, 768)
-        finish_on_vector(768, 896)
-        finish(896, 1024)
+        relu_on_scalar(0, 512)
+        relu_on_scalar(512, 768)
+        relu_on_vector(768, 896)
+        relu_on_scalar(896, 1024)
 
         terms = [keep.tile([P, V], F32, name=f"term{d}") for d in range(D)]
         blocks = V // P
-        turned = [psum.tile([P, V], F32, name=f"bank{(5 + c) % 8}") for c in range(blocks)]
-        back = {c0: psum.tile([P, V], F32, name=f"bank{bank}") for c0, bank in ((0, 1), (2, 2), (3, 4))}
+        turned = [bank(n) for n in (5, 6, 7, 0)]
+        back = {c0: bank(n) for (c0, c1), n in zip(PIECES, (1, 2, 4))}
         partial = [keep.tile([P, P], F32, name=f"partial{c}") for c in range(blocks)]
 
-        def neighbour(d, v0=0, v1=V):
-            idx = offsets[d][:, v0 // 16 : v1 // 16]
-            nc.vector.tensor_tensor(terms[d][:, v0:v1], y[:].indirect(idx), gates[d][:, v0:v1], MULT)
+        def neighbour(d, v0, v1):
+            entries = offsets[d][:, v0 // 16 : v1 // 16]
+            nc.vector.tensor_tensor(terms[d][:, v0:v1], y[:].indirect(entries), gates[d][:, v0:v1], MULT)
 
         def accumulate(d, c):
             nc.tensor.matmul(
@@ -158,10 +162,10 @@ def tile_picked_agg_lin_relu_sub_l_kernel(
             nc.tensor.transpose(back[c0][:, (c - c0) * P : (c - c0 + 1) * P], partial[c][:], ident[:])
 
         for d in range(D - 2):
-            neighbour(d)
+            neighbour(d, 0, V)
             for c in range(blocks):
                 accumulate(d, c)
-        for c0, c1 in ((0, 2), (2, 3), (3, 4)):
+        for c0, c1 in PIECES:
             neighbour(D - 2, c0 * P, c1 * P)
             for c in range(c0, c1):
                 accumulate(D - 2, c)
@@ -169,9 +173,8 @@ def tile_picked_agg_lin_relu_sub_l_kernel(
                 turn_back(c0, c)
         for h in range(2):
             neighbour(D - 1, h * HALF, (h + 1) * HALF)
-        for c0, c1 in ((0, 2), (2, 3), (3, 4)):
+        for c0, c1 in PIECES:
             cols = slice(c0 * P, c1 * P)
             result = keep.tile([P, (c1 - c0) * P], F32, name=f"result{c0}")
-            turned_back = back[c0][:, 0 : (c1 - c0) * P]
-            nc.vector.tensor_tensor(result[:], turned_back, terms[D - 1][:, cols], ADD)
+            nc.vector.tensor_tensor(result[:], back[c0][:, 0 : (c1 - c0) * P], terms[D - 1][:, cols], ADD)
             nc.sync.dma_start(out=out[:, cols], in_=result[:])

@@ -22,7 +22,7 @@ MULT = mybir.AluOpType.mult
 ADD = mybir.AluOpType.add
 MAX = mybir.AluOpType.max
 
-LOADS = ((0, 512), (512, 832), (832, 1024))
+LOADS = ((0, 512), (512, 768), (768, 1024))
 PIECES = ((0, 2), (2, 3), (3, 4))
 HALF = V // 2
 
@@ -124,10 +124,10 @@ def tile_picked_agg_lin_relu_sub_l_kernel(
         copy_on_scalar(288, 512)
         project(0, 256, 0)
         project(256, 512, 0)
-        copy_on_vector(512, 704)
-        copy_on_scalar(704, 832)
+        copy_on_vector(512, 672)
+        copy_on_scalar(672, 768)
         project(512, 768, 512)
-        copy_on_vector(832, 896)
+        copy_on_vector(768, 896)
         copy_on_vector(896, 928)
         copy_on_scalar(928, 1024)
         project(768, 896, 768)

@@ -18,6 +18,7 @@ U16 = mybir.dt.uint16
 U8 = mybir.dt.uint8
 FP8X4 = mybir.dt.float8_e4m3fn_x4
 RELU = mybir.ActivationFunctionType.Relu
+COPY = mybir.ActivationFunctionType.Copy
 MULT = mybir.AluOpType.mult
 ADD = mybir.AluOpType.add
 MAX = mybir.AluOpType.max
@@ -25,6 +26,7 @@ MAX = mybir.AluOpType.max
 LOADS = ((0, 512), (512, 768), (768, 1024))
 PIECES = ((0, 2), (2, 3), (3, 4))
 HALF = V // 2
+ON_SCALAR = (1, 3, 4)
 
 
 def tile_picked_agg_lin_relu_sub_l_kernel(
@@ -71,8 +73,13 @@ def tile_picked_agg_lin_relu_sub_l_kernel(
         nc.sync.dma_start(out=bias[:], in_=b)
 
         gates = [keep.tile([P, V], F32, name=f"gate{d}") for d in range(D)]
-        for d, pos in enumerate((pos1, pos2, pos3, pos4, pos5, pos6)):
-            nc.sync.dma_start(out=offsets[d][:], in_=pos)
+        positions = (pos1, pos2, pos3, pos4, pos5, pos6)
+        early = {d - 1: d for d in ON_SCALAR}
+        for d in range(D):
+            if d in early:
+                nc.sync.dma_start(out=offsets[early[d]][:], in_=positions[early[d]])
+            if d not in ON_SCALAR:
+                nc.sync.dma_start(out=offsets[d][:], in_=positions[d])
             nc.sync.dma_start(out=gates[d][:], in_=gate[d])
 
         grouped = keep.tile([P, T, PACK], BF16, align_bytes=64)
@@ -138,6 +145,7 @@ def tile_picked_agg_lin_relu_sub_l_kernel(
         relu_on_scalar(896, 1024)
 
         terms = [keep.tile([P, V], F32, name=f"term{d}") for d in range(D)]
+        picked = {d: keep.tile([P, V], F32, name=f"picked{d}") for d in ON_SCALAR}
         blocks = V // P
         turned = [bank(n) for n in (5, 6, 7, 0)]
         back = {c0: bank(n) for (c0, c1), n in zip(PIECES, (1, 2, 4))}
@@ -145,7 +153,11 @@ def tile_picked_agg_lin_relu_sub_l_kernel(
 
         def neighbour(d, v0, v1):
             entries = offsets[d][:, v0 // 16 : v1 // 16]
-            nc.vector.tensor_tensor(terms[d][:, v0:v1], y[:].indirect(entries), gates[d][:, v0:v1], MULT)
+            if d in ON_SCALAR:
+                nc.scalar.activation(picked[d][:, v0:v1], y[:].indirect(entries), COPY)
+                nc.vector.tensor_tensor(terms[d][:, v0:v1], picked[d][:, v0:v1], gates[d][:, v0:v1], MULT)
+            else:
+                nc.vector.tensor_tensor(terms[d][:, v0:v1], y[:].indirect(entries), gates[d][:, v0:v1], MULT)
 
         def accumulate(d, c):
             nc.tensor.matmul(

@@ -26,7 +26,7 @@ MAX = mybir.AluOpType.max
 LOADS = ((0, 512), (512, 768), (768, 1024))
 PIECES = ((0, 2), (2, 3), (3, 4))
 HALF = V // 2
-ON_SCALAR = (1, 3, 4)
+ON_SCALAR = (2, 3, 4)
 
 
 def tile_picked_agg_lin_relu_sub_l_kernel(
@@ -74,7 +74,7 @@ def tile_picked_agg_lin_relu_sub_l_kernel(
 
         gates = [keep.tile([P, V], F32, name=f"gate{d}") for d in range(D)]
         positions = (pos1, pos2, pos3, pos4, pos5, pos6)
-        early = {d - 1: d for d in ON_SCALAR}
+        early = {d - 2: d for d in ON_SCALAR}
         for d in range(D):
             if d in early:
                 nc.sync.dma_start(out=offsets[early[d]][:], in_=positions[early[d]])

@@ -74,11 +74,11 @@ def tile_picked_agg_lin_relu_sub_l_kernel(
 
         gates = [keep.tile([P, V], F32, name=f"gate{d}") for d in range(D)]
         positions = (pos1, pos2, pos3, pos4, pos5, pos6)
-        early = {d - 2: d for d in ON_SCALAR}
+        early = {d - 2: d for d in range(2, D)}
         for d in range(D):
             if d in early:
                 nc.sync.dma_start(out=offsets[early[d]][:], in_=positions[early[d]])
-            if d not in ON_SCALAR:
+            if d < 2:
                 nc.sync.dma_start(out=offsets[d][:], in_=positions[d])
             nc.sync.dma_start(out=gates[d][:], in_=gate[d])
 
@@ -145,7 +145,7 @@ def tile_picked_agg_lin_relu_sub_l_kernel(
         relu_on_scalar(896, 1024)
 
         terms = [keep.tile([P, V], F32, name=f"term{d}") for d in range(D)]
-        picked = {d: keep.tile([P, V], F32, name=f"picked{d}") for d in ON_SCALAR}
+        picked = {d: keep.tile([P, V], F32, name=f"picked{d}") for d in range(2, D)}
         blocks = V // P
         turned = [bank(n) for n in (5, 6, 7, 0)]
         back = {c0: bank(n) for (c0, c1), n in zip(PIECES, (1, 2, 4))}
@@ -153,7 +153,7 @@ def tile_picked_agg_lin_relu_sub_l_kernel(
 
         def neighbour(d, v0, v1):
             entries = offsets[d][:, v0 // 16 : v1 // 16]
-            if d in ON_SCALAR:
+            if d in ON_SCALAR or (d == D - 1 and v0 >= HALF):
                 nc.scalar.activation(picked[d][:, v0:v1], y[:].indirect(entries), COPY)
                 nc.vector.tensor_tensor(terms[d][:, v0:v1], picked[d][:, v0:v1], gates[d][:, v0:v1], MULT)
             else:

@@ -26,7 +26,6 @@ MAX = mybir.AluOpType.max
 LOADS = ((0, 512), (512, 768), (768, 1024))
 PIECES = ((0, 2), (2, 3), (3, 4))
 HALF = V // 2
-ON_SCALAR = (2, 3, 4)
 
 
 def tile_picked_agg_lin_relu_sub_l_kernel(
@@ -72,15 +71,34 @@ def tile_picked_agg_lin_relu_sub_l_kernel(
         load_x(*LOADS[2])
         nc.sync.dma_start(out=bias[:], in_=b)
 
-        gates = [keep.tile([P, V], F32, name=f"gate{d}") for d in range(D)]
+        gates = {d: keep.tile([P, V], F32, name=f"gate{d}") for d in (0, 1, 4, 5)}
         positions = (pos1, pos2, pos3, pos4, pos5, pos6)
-        early = {d - 2: d for d in range(2, D)}
-        for d in range(D):
-            if d in early:
-                nc.sync.dma_start(out=offsets[early[d]][:], in_=positions[early[d]])
-            if d < 2:
-                nc.sync.dma_start(out=offsets[d][:], in_=positions[d])
+
+        def load_list(d):
+            nc.sync.dma_start(out=offsets[d][:], in_=positions[d])
+
+        def load_gate(d):
             nc.sync.dma_start(out=gates[d][:], in_=gate[d])
+
+        load_list(1)
+        load_list(0)
+        load_gate(0)
+        load_list(3)
+        load_gate(1)
+        load_list(2)
+        load_list(4)
+        paired = [keep.tile([P, 2, HALF], F32, name=f"paired{h}") for h in range(2)]
+        for h in range(2):
+            nc.sync.dma_start(out=paired[h][:], in_=gate[2:4, :, h * HALF : (h + 1) * HALF].rearrange("d m v -> m d v"))
+        load_list(5)
+        load_gate(4)
+        load_gate(5)
+
+        def weights(d, v0, v1):
+            if d in gates:
+                return gates[d][:, v0:v1]
+            h = v0 // HALF
+            return paired[h][:, d - 2, v0 - h * HALF : v1 - h * HALF]
 
         grouped = keep.tile([P, T, PACK], BF16, align_bytes=64)
         x_codes = keep.tile([P, T], U32, align_bytes=64)
@@ -145,48 +163,70 @@ def tile_picked_agg_lin_relu_sub_l_kernel(
         relu_on_scalar(896, 1024)
 
         terms = [keep.tile([P, V], F32, name=f"term{d}") for d in range(D)]
-        picked = {d: keep.tile([P, V], F32, name=f"picked{d}") for d in range(2, D)}
+        picked = {d: keep.tile([P, V], F32, name=f"picked{d}") for d in (1, 3, 4, 5)}
         blocks = V // P
         turned = [bank(n) for n in (5, 6, 7, 0)]
         back = {c0: bank(n) for (c0, c1), n in zip(PIECES, (1, 2, 4))}
         partial = [keep.tile([P, P], F32, name=f"partial{c}") for c in range(blocks)]
 
-        def neighbour(d, v0, v1):
-            entries = offsets[d][:, v0 // 16 : v1 // 16]
-            if d in ON_SCALAR or (d == D - 1 and v0 >= HALF):
-                nc.scalar.activation(picked[d][:, v0:v1], y[:].indirect(entries), COPY)
-                nc.vector.tensor_tensor(terms[d][:, v0:v1], picked[d][:, v0:v1], gates[d][:, v0:v1], MULT)
-            else:
-                nc.vector.tensor_tensor(terms[d][:, v0:v1], y[:].indirect(entries), gates[d][:, v0:v1], MULT)
+        def entries(d, v0, v1):
+            return y[:].indirect(offsets[d][:, v0 // 16 : v1 // 16])
 
-        def accumulate(d, c):
-            nc.tensor.matmul(
-                turned[c][:, 0:P],
-                lhsT=terms[d][:, c * P : (c + 1) * P],
-                rhs=ident[:],
-                is_transpose=True,
-                start=(d == 0),
-                stop=(d == D - 2),
-            )
+        def fused(d, v0, v1):
+            nc.vector.tensor_tensor(terms[d][:, v0:v1], entries(d, v0, v1), weights(d, v0, v1), MULT)
+
+        def pick(d, v0, v1):
+            nc.scalar.activation(picked[d][:, v0:v1], entries(d, v0, v1), COPY)
+
+        def weigh(d, v0, v1):
+            nc.vector.tensor_tensor(terms[d][:, v0:v1], picked[d][:, v0:v1], weights(d, v0, v1), MULT)
+
+        summed = [0] * blocks
+
+        def accumulate(d, v0, v1):
+            for c in range(v0 // P, v1 // P):
+                nc.tensor.matmul(
+                    turned[c][:, 0:P],
+                    lhsT=terms[d][:, c * P : (c + 1) * P],
+                    rhs=ident[:],
+                    is_transpose=True,
+                    start=(summed[c] == 0),
+                    stop=(summed[c] == D - 2),
+                )
+                summed[c] = summed[c] + 1
 
         def turn_back(c0, c):
             nc.scalar.copy(partial[c][:], turned[c][:, 0:P])
             nc.tensor.transpose(back[c0][:, (c - c0) * P : (c - c0 + 1) * P], partial[c][:], ident[:])
 
-        for d in range(D - 2):
-            neighbour(d, 0, V)
-            for c in range(blocks):
-                accumulate(d, c)
+        for d in (1, 3):
+            pick(d, 0, HALF)
+            pick(d, HALF, V)
         for c0, c1 in PIECES:
-            neighbour(D - 2, c0 * P, c1 * P)
-            for c in range(c0, c1):
-                accumulate(D - 2, c)
+            pick(4, c0 * P, c1 * P)
+        pick(5, HALF, V)
+        for step, d, v0, v1 in (
+            (fused, 0, 0, HALF),
+            (fused, 0, HALF, V),
+            (weigh, 1, 0, HALF),
+            (weigh, 1, HALF, V),
+            (fused, 2, 0, HALF),
+            (weigh, 3, 0, HALF),
+            (fused, 2, HALF, V),
+            (weigh, 3, HALF, V),
+        ):
+            step(d, v0, v1)
+            accumulate(d, v0, v1)
+        for c0, c1 in PIECES:
+            weigh(4, c0 * P, c1 * P)
+            accumulate(4, c0 * P, c1 * P)
+        for c0, c1 in PIECES:
             for c in range(c0, c1):
                 turn_back(c0, c)
-        for h in range(2):
-            neighbour(D - 1, h * HALF, (h + 1) * HALF)
+        fused(5, 0, HALF)
+        weigh(5, HALF, V)
         for c0, c1 in PIECES:
             cols = slice(c0 * P, c1 * P)
             result = keep.tile([P, (c1 - c0) * P], F32, name=f"result{c0}")
-            nc.vector.tensor_tensor(result[:], back[c0][:, 0 : (c1 - c0) * P], terms[D - 1][:, cols], ADD)
+            nc.vector.tensor_tensor(result[:], back[c0][:, 0 : (c1 - c0) * P], terms[5][:, cols], ADD)
             nc.sync.dma_start(out=out[:, cols], in_=result[:])

@@ -53,25 +53,24 @@ def tile_picked_agg_lin_relu_sub_l_kernel(
         bias = keep.tile([P, 1], F32)
 
         x_rows = xT.rearrange("(p j) t -> p j t", j=PACK)
-        raws = []
+        raws = {}
 
-        def load_x(t0, t1):
-            raw = keep.tile([P, PACK, t1 - t0], F32, name=f"raw{len(raws)}")
-            nc.sync.dma_start(out=raw[:], in_=x_rows[:, :, t0:t1])
-            raws.append(raw)
+        def load_x(j0, t0, t1):
+            raws[j0, t0, t1] = keep.tile([P, 2, t1 - t0], F32, name=f"raw{len(raws)}")
+            nc.sync.dma_start(out=raws[j0, t0, t1][:], in_=x_rows[:, j0 : j0 + 2, t0:t1])
 
-        load_x(*LOADS[0])
+        load_x(0, 0, T)
         scale_rows = w_scales.rearrange("a q m -> (a q) m")
         for quadrant in range(4):
             nc.sync.dma_start(
                 out=w_scale[32 * quadrant : 32 * quadrant + 4, :].bitcast(I32),
                 in_=scale_rows[4 * quadrant : 4 * quadrant + 4, :].bitcast(I32),
             )
-        load_x(*LOADS[1])
-        load_x(*LOADS[2])
+        for t0, t1 in LOADS:
+            load_x(2, t0, t1)
         nc.sync.dma_start(out=bias[:], in_=b)
 
-        gates = {d: keep.tile([P, V], F32, name=f"gate{d}") for d in (0, 1, 4, 5)}
+        gates = {d: keep.tile([P, V], F32, name=f"gate{d}") for d in (0, 1)}
         positions = (pos1, pos2, pos3, pos4, pos5, pos6)
 
         def load_list(d):
@@ -91,12 +90,14 @@ def tile_picked_agg_lin_relu_sub_l_kernel(
         for h in range(2):
             nc.sync.dma_start(out=paired[h][:], in_=gate[2:4, :, h * HALF : (h + 1) * HALF].rearrange("d m v -> m d v"))
         load_list(5)
-        load_gate(4)
-        load_gate(5)
+        late = keep.tile([P, 2, V], F32)
+        nc.sync.dma_start(out=late[:], in_=gate[4:6].rearrange("d m v -> m d v"))
 
         def weights(d, v0, v1):
             if d in gates:
                 return gates[d][:, v0:v1]
+            if d >= 4:
+                return late[:, d - 4, v0:v1]
             h = v0 // HALF
             return paired[h][:, d - 2, v0 - h * HALF : v1 - h * HALF]
 
@@ -106,19 +107,19 @@ def tile_picked_agg_lin_relu_sub_l_kernel(
         y = keep.tile([P, T], F32)
         products = {}
 
-        def loaded(t0, t1):
-            for raw, (l0, l1) in zip(raws, LOADS):
-                if l0 <= t0 and t1 <= l1:
+        def loaded(j0, t0, t1):
+            for (j, l0, l1), raw in raws.items():
+                if j == j0 and l0 <= t0 and t1 <= l1:
                     return raw[:, :, t0 - l0 : t1 - l0].rearrange("p j (c i) -> p c j i", i=LINE)
 
-        def laid(t0, t1):
-            return grouped[:, t0:t1, :].rearrange("p (c i) j -> p c j i", i=LINE)
+        def laid(j0, t0, t1):
+            return grouped[:, t0:t1, j0 : j0 + 2].rearrange("p (c i) j -> p c j i", i=LINE)
 
-        def copy_on_vector(t0, t1):
-            nc.vector.tensor_copy(laid(t0, t1), loaded(t0, t1))
+        def copy_on_vector(j0, t0, t1):
+            nc.vector.tensor_copy(laid(j0, t0, t1), loaded(j0, t0, t1))
 
-        def copy_on_scalar(t0, t1):
-            nc.scalar.copy(laid(t0, t1), loaded(t0, t1))
+        def copy_on_scalar(j0, t0, t1):
+            nc.scalar.copy(laid(j0, t0, t1), loaded(j0, t0, t1))
 
         def project(t0, t1, first):
             nc.vector.quantize_mx(
@@ -144,17 +145,17 @@ def tile_picked_agg_lin_relu_sub_l_kernel(
         def relu_on_vector(t0, t1):
             nc.vector.tensor_scalar(y[:, t0:t1], products[t0][:, 0 : t1 - t0], bias[:], 0.0, ADD, MAX)
 
-        copy_on_vector(0, 256)
-        copy_on_vector(256, 288)
-        copy_on_scalar(288, 512)
+        copy_on_vector(0, 0, 672)
+        copy_on_scalar(0, 672, 1024)
+        copy_on_vector(2, 0, 256)
+        copy_on_vector(2, 256, 320)
+        copy_on_scalar(2, 320, 512)
         project(0, 256, 0)
         project(256, 512, 0)
-        copy_on_vector(512, 672)
-        copy_on_scalar(672, 768)
+        copy_on_scalar(2, 512, 768)
+        copy_on_vector(2, 768, 896)
+        copy_on_vector(2, 896, 1024)
         project(512, 768, 512)
-        copy_on_vector(768, 896)
-        copy_on_vector(896, 928)
-        copy_on_scalar(928, 1024)
         project(768, 896, 768)
         project(896, 1024, 896)
         relu_on_scalar(0, 512)

@@ -152,9 +152,10 @@ def tile_picked_agg_lin_relu_sub_l_kernel(
         copy_on_scalar(2, 320, 512)
         project(0, 256, 0)
         project(256, 512, 0)
-        copy_on_scalar(2, 512, 768)
+        copy_on_vector(2, 512, 576)
+        copy_on_scalar(2, 576, 768)
         copy_on_vector(2, 768, 896)
-        copy_on_vector(2, 896, 1024)
+        copy_on_scalar(2, 896, 1024)
         project(512, 768, 512)
         project(768, 896, 768)
         project(896, 1024, 896)

@@ -148,15 +148,17 @@ def tile_picked_agg_lin_relu_sub_l_kernel(
         copy_on_vector(0, 0, 672)
         copy_on_scalar(0, 672, 1024)
         copy_on_vector(2, 0, 256)
-        copy_on_vector(2, 256, 320)
-        copy_on_scalar(2, 320, 512)
+        copy_on_vector(2, 256, 384)
+        copy_on_scalar(2, 384, 512)
         project(0, 256, 0)
         project(256, 512, 0)
-        copy_on_vector(2, 512, 576)
-        copy_on_scalar(2, 576, 768)
+        copy_on_scalar(2, 512, 640)
+        copy_on_scalar(2, 640, 768)
         copy_on_vector(2, 768, 896)
-        copy_on_scalar(2, 896, 1024)
-        project(512, 768, 512)
+        copy_on_vector(2, 896, 928)
+        copy_on_scalar(2, 928, 1024)
+        project(512, 640, 512)
+        project(640, 768, 512)
         project(768, 896, 768)
         project(896, 1024, 896)
         relu_on_scalar(0, 512)

@@ -24,7 +24,7 @@ ADD = mybir.AluOpType.add
 MAX = mybir.AluOpType.max
 
 LOADS = ((0, 512), (512, 768), (768, 1024))
-PIECES = ((0, 2), (2, 3), (3, 4))
+PIECES = ((0, 2), (3, 4), (2, 3))
 HALF = V // 2
 
 
@@ -70,7 +70,7 @@ def tile_picked_agg_lin_relu_sub_l_kernel(
             load_x(2, t0, t1)
         nc.sync.dma_start(out=bias[:], in_=b)
 
-        gates = {d: keep.tile([P, V], F32, name=f"gate{d}") for d in (0, 1)}
+        gates = {d: keep.tile([P, V], F32, name=f"gate{d}") for d in (0, 1, 5)}
         positions = (pos1, pos2, pos3, pos4, pos5, pos6)
 
         def load_list(d):
@@ -85,19 +85,23 @@ def tile_picked_agg_lin_relu_sub_l_kernel(
         load_list(3)
         load_gate(1)
         load_list(2)
-        load_list(4)
         paired = [keep.tile([P, 2, HALF], F32, name=f"paired{h}") for h in range(2)]
-        for h in range(2):
+
+        def load_pair(h):
             nc.sync.dma_start(out=paired[h][:], in_=gate[2:4, :, h * HALF : (h + 1) * HALF].rearrange("d m v -> m d v"))
+
+        load_pair(0)
+        load_list(4)
+        load_pair(1)
+        column = keep.tile([P, V // P, 8], F32)
+        with nc.allow_non_contiguous_dma(reason="one weight a partition and block"):
+            nc.sync.dma_start(out=column[:, :, 0:1], in_=gate[4, 0:1, :].rearrange("o (c p) -> p c o", p=P))
         load_list(5)
-        late = keep.tile([P, 2, V], F32)
-        nc.sync.dma_start(out=late[:], in_=gate[4:6].rearrange("d m v -> m d v"))
+        load_gate(5)
 
         def weights(d, v0, v1):
             if d in gates:
                 return gates[d][:, v0:v1]
-            if d >= 4:
-                return late[:, d - 4, v0:v1]
             h = v0 // HALF
             return paired[h][:, d - 2, v0 - h * HALF : v1 - h * HALF]
 
@@ -166,12 +170,13 @@ def tile_picked_agg_lin_relu_sub_l_kernel(
         relu_on_vector(768, 896)
         relu_on_scalar(896, 1024)
 
-        terms = [keep.tile([P, V], F32, name=f"term{d}") for d in range(D)]
-        picked = {d: keep.tile([P, V], F32, name=f"picked{d}") for d in (1, 3, 4, 5)}
-        blocks = V // P
-        turned = [bank(n) for n in (5, 6, 7, 0)]
-        back = {c0: bank(n) for (c0, c1), n in zip(PIECES, (1, 2, 4))}
-        partial = [keep.tile([P, P], F32, name=f"partial{c}") for c in range(blocks)]
+        terms = {d: keep.tile([P, V], F32, name=f"term{d}") for d in (0, 1, 2, 3, 5)}
+        picked = {d: keep.tile([P, V], F32, name=f"picked{d}") for d in (1, 3, 4)}
+        turned = {c0: bank(n) for (c0, c1), n in zip(PIECES, (4, 5, 6))}
+        plain = {c0: bank(n) for (c0, c1), n in zip(PIECES, (7, 0, 1))}
+        partial = {c0: keep.tile([P, (c1 - c0) * P], F32, name=f"partial{c0}") for c0, c1 in PIECES}
+        scaled = [keep.tile([P, P], F32, name=f"scaled{c}") for c in range(V // P)]
+        piece_of = {c: (c0, c1) for c0, c1 in PIECES for c in range(c0, c1)}
 
         def entries(d, v0, v1):
             return y[:].indirect(offsets[d][:, v0 // 16 : v1 // 16])
@@ -185,30 +190,25 @@ def tile_picked_agg_lin_relu_sub_l_kernel(
         def weigh(d, v0, v1):
             nc.vector.tensor_tensor(terms[d][:, v0:v1], picked[d][:, v0:v1], weights(d, v0, v1), MULT)
 
-        summed = [0] * blocks
+        passes = {}
 
-        def accumulate(d, v0, v1):
-            for c in range(v0 // P, v1 // P):
-                nc.tensor.matmul(
-                    turned[c][:, 0:P],
-                    lhsT=terms[d][:, c * P : (c + 1) * P],
-                    rhs=ident[:],
-                    is_transpose=True,
-                    start=(summed[c] == 0),
-                    stop=(summed[c] == D - 2),
-                )
-                summed[c] = summed[c] + 1
+        def turn(banks, name, count, c, block):
+            c0, c1 = piece_of[c]
+            done = passes.get((name, c0), 0)
+            nc.tensor.matmul(
+                banks[c0][:, (c - c0) * P : (c - c0 + 1) * P],
+                lhsT=block,
+                rhs=ident[:],
+                is_transpose=True,
+                start=(done == 0),
+                stop=(done == count * (c1 - c0) - 1),
+            )
+            passes[name, c0] = done + 1
 
-        def turn_back(c0, c):
-            nc.scalar.copy(partial[c][:], turned[c][:, 0:P])
-            nc.tensor.transpose(back[c0][:, (c - c0) * P : (c - c0 + 1) * P], partial[c][:], ident[:])
-
-        for d in (1, 3):
-            pick(d, 0, HALF)
-            pick(d, HALF, V)
-        for c0, c1 in PIECES:
-            pick(4, c0 * P, c1 * P)
-        pick(5, HALF, V)
+        pick(1, 0, HALF)
+        pick(1, HALF, V)
+        pick(3, 0, HALF)
+        pick(3, HALF, HALF + P)
         for step, d, v0, v1 in (
             (fused, 0, 0, HALF),
             (fused, 0, HALF, V),
@@ -216,21 +216,33 @@ def tile_picked_agg_lin_relu_sub_l_kernel(
             (weigh, 1, HALF, V),
             (fused, 2, 0, HALF),
             (weigh, 3, 0, HALF),
-            (fused, 2, HALF, V),
-            (weigh, 3, HALF, V),
+            (fused, 3, HALF + P, V),
+            (fused, 2, HALF + P, V),
+            (fused, 2, HALF, HALF + P),
+            (weigh, 3, HALF, HALF + P),
         ):
             step(d, v0, v1)
-            accumulate(d, v0, v1)
+            for c in range(v0 // P, v1 // P):
+                turn(turned, "turned", 4, c, terms[d][:, c * P : (c + 1) * P])
         for c0, c1 in PIECES:
-            weigh(4, c0 * P, c1 * P)
-            accumulate(4, c0 * P, c1 * P)
+            pick(4, c0 * P, c1 * P)
+            for c in range(c0, c1):
+                turn(plain, "plain", 1, c, picked[4][:, c * P : (c + 1) * P])
+        back = {c0: bank(n) for (c0, c1), n in zip(PIECES, (2, 3, 4))}
         for c0, c1 in PIECES:
             for c in range(c0, c1):
-                turn_back(c0, c)
+                nc.scalar.activation(
+                    scaled[c][:], plain[c0][:, (c - c0) * P : (c - c0 + 1) * P], COPY, scale=column[:, c, 0:1]
+                )
+                turn(back, "back", 2, c, scaled[c][:])
+            nc.scalar.copy(partial[c0][:], turned[c0][:, 0 : (c1 - c0) * P])
+            for c in range(c0, c1):
+                turn(back, "back", 2, c, partial[c0][:, (c - c0) * P : (c - c0 + 1) * P])
         fused(5, 0, HALF)
-        weigh(5, HALF, V)
+        fused(5, HALF, V)
+        result = keep.tile([P, V], F32)
         for c0, c1 in PIECES:
             cols = slice(c0 * P, c1 * P)
-            result = keep.tile([P, (c1 - c0) * P], F32, name=f"result{c0}")
-            nc.vector.tensor_tensor(result[:], back[c0][:, 0 : (c1 - c0) * P], terms[5][:, cols], ADD)
-            nc.sync.dma_start(out=out[:, cols], in_=result[:])
+            nc.vector.tensor_tensor(result[:, cols], back[c0][:, 0 : (c1 - c0) * P], terms[5][:, cols], ADD)
+        for h in range(2):
+            nc.sync.dma_start(out=out[:, h * HALF : (h + 1) * HALF], in_=result[:, h * HALF : (h + 1) * HALF])

@@ -24,7 +24,7 @@ ADD = mybir.AluOpType.add
 MAX = mybir.AluOpType.max
 
 LOADS = ((0, 512), (512, 768), (768, 1024))
-PIECES = ((0, 2), (3, 4), (2, 3))
+PIECES = ((0, 2), (2, 3), (3, 4))
 HALF = V // 2
 
 
@@ -70,40 +70,31 @@ def tile_picked_agg_lin_relu_sub_l_kernel(
             load_x(2, t0, t1)
         nc.sync.dma_start(out=bias[:], in_=b)
 
-        gates = {d: keep.tile([P, V], F32, name=f"gate{d}") for d in (0, 1, 5)}
         positions = (pos1, pos2, pos3, pos4, pos5, pos6)
+        gates = {}
 
         def load_list(d):
             nc.sync.dma_start(out=offsets[d][:], in_=positions[d])
 
-        def load_gate(d):
-            nc.sync.dma_start(out=gates[d][:], in_=gate[d])
+        def load_gates(d0, d1):
+            joint = keep.tile([P, d1 - d0, V], F32, name=f"gates{d0}")
+            nc.sync.dma_start(out=joint[:], in_=gate[d0:d1].rearrange("d m v -> m d v"))
+            for d in range(d0, d1):
+                gates[d] = joint[:, d - d0, :]
 
-        load_list(1)
-        load_list(0)
-        load_gate(0)
-        load_list(3)
-        load_gate(1)
-        load_list(2)
-        paired = [keep.tile([P, 2, HALF], F32, name=f"paired{h}") for h in range(2)]
-
-        def load_pair(h):
-            nc.sync.dma_start(out=paired[h][:], in_=gate[2:4, :, h * HALF : (h + 1) * HALF].rearrange("d m v -> m d v"))
-
-        load_pair(0)
         load_list(4)
-        load_pair(1)
+        load_list(0)
+        load_gates(0, 1)
+        load_list(1)
+        load_list(2)
+        load_gates(1, 2)
+        load_list(3)
+        load_gates(2, 4)
         column = keep.tile([P, V // P, 8], F32)
         with nc.allow_non_contiguous_dma(reason="one weight a partition and block"):
             nc.sync.dma_start(out=column[:, :, 0:1], in_=gate[4, 0:1, :].rearrange("o (c p) -> p c o", p=P))
         load_list(5)
-        load_gate(5)
-
-        def weights(d, v0, v1):
-            if d in gates:
-                return gates[d][:, v0:v1]
-            h = v0 // HALF
-            return paired[h][:, d - 2, v0 - h * HALF : v1 - h * HALF]
+        load_gates(5, 6)
 
         grouped = keep.tile([P, T, PACK], BF16, align_bytes=64)
         x_codes = keep.tile([P, T], U32, align_bytes=64)
@@ -170,79 +161,78 @@ def tile_picked_agg_lin_relu_sub_l_kernel(
         relu_on_vector(768, 896)
         relu_on_scalar(896, 1024)
 
+        blocks = V // P
         terms = {d: keep.tile([P, V], F32, name=f"term{d}") for d in (0, 1, 2, 3, 5)}
-        picked = {d: keep.tile([P, V], F32, name=f"picked{d}") for d in (1, 3, 4)}
-        turned = {c0: bank(n) for (c0, c1), n in zip(PIECES, (4, 5, 6))}
-        plain = {c0: bank(n) for (c0, c1), n in zip(PIECES, (7, 0, 1))}
-        partial = {c0: keep.tile([P, (c1 - c0) * P], F32, name=f"partial{c0}") for c0, c1 in PIECES}
-        scaled = [keep.tile([P, P], F32, name=f"scaled{c}") for c in range(V // P)]
+        picked = {d: keep.tile([P, V], F32, name=f"picked{d}") for d in (2, 3, 4)}
+        turned = [bank(n) for n in (4, 5, 6, 7)]
+        plain = bank(0)
+        back = {c0: bank(n) for (c0, c1), n in zip(PIECES, (1, 2, 3))}
+        partial = [keep.tile([P, P], F32, name=f"partial{c}") for c in range(blocks)]
+        scaled = [keep.tile([P, P], F32, name=f"scaled{c}") for c in range(blocks)]
         piece_of = {c: (c0, c1) for c0, c1 in PIECES for c in range(c0, c1)}
 
-        def entries(d, v0, v1):
-            return y[:].indirect(offsets[d][:, v0 // 16 : v1 // 16])
+        def cols(c0, c1):
+            return slice(c0 * P, c1 * P)
 
-        def fused(d, v0, v1):
-            nc.vector.tensor_tensor(terms[d][:, v0:v1], entries(d, v0, v1), weights(d, v0, v1), MULT)
+        def entries(d, c0, c1):
+            return y[:].indirect(offsets[d][:, c0 * P // 16 : c1 * P // 16])
 
-        def pick(d, v0, v1):
-            nc.scalar.activation(picked[d][:, v0:v1], entries(d, v0, v1), COPY)
+        def fused(d, c0, c1):
+            nc.vector.tensor_tensor(terms[d][:, cols(c0, c1)], entries(d, c0, c1), gates[d][:, cols(c0, c1)], MULT)
 
-        def weigh(d, v0, v1):
-            nc.vector.tensor_tensor(terms[d][:, v0:v1], picked[d][:, v0:v1], weights(d, v0, v1), MULT)
+        def pick(d, c0, c1):
+            nc.scalar.activation(picked[d][:, cols(c0, c1)], entries(d, c0, c1), COPY)
+
+        def weigh(d, c0, c1):
+            nc.vector.tensor_tensor(terms[d][:, cols(c0, c1)], picked[d][:, cols(c0, c1)], gates[d][:, cols(c0, c1)], MULT)
 
         passes = {}
 
-        def turn(banks, name, count, c, block):
-            c0, c1 = piece_of[c]
-            done = passes.get((name, c0), 0)
+        def turn(name, count, target, block):
+            done = passes.get(name, 0)
             nc.tensor.matmul(
-                banks[c0][:, (c - c0) * P : (c - c0 + 1) * P],
-                lhsT=block,
-                rhs=ident[:],
-                is_transpose=True,
-                start=(done == 0),
-                stop=(done == count * (c1 - c0) - 1),
+                target, lhsT=block, rhs=ident[:], is_transpose=True, start=(done == 0), stop=(done == count - 1)
             )
-            passes[name, c0] = done + 1
+            passes[name] = done + 1
 
-        pick(1, 0, HALF)
-        pick(1, HALF, V)
-        pick(3, 0, HALF)
-        pick(3, HALF, HALF + P)
-        for step, d, v0, v1 in (
-            (fused, 0, 0, HALF),
-            (fused, 0, HALF, V),
-            (weigh, 1, 0, HALF),
-            (weigh, 1, HALF, V),
-            (fused, 2, 0, HALF),
-            (weigh, 3, 0, HALF),
-            (fused, 3, HALF + P, V),
-            (fused, 2, HALF + P, V),
-            (fused, 2, HALF, HALF + P),
-            (weigh, 3, HALF, HALF + P),
+        def turn_back(c, block):
+            c0, c1 = piece_of[c]
+            turn(("back", c0), 2 * (c1 - c0), back[c0][:, cols(c - c0, c - c0 + 1)], block)
+
+        for c0, c1 in PIECES:
+            pick(4, c0, c1)
+            for c in range(c0, c1):
+                turn("plain", blocks, plain[:, cols(c, c + 1)], picked[4][:, cols(c, c + 1)])
+        pick(2, 0, 2)
+        pick(2, 2, 4)
+        pick(3, 1, 2)
+        pick(3, 2, 4)
+        for step, d, c0, c1 in (
+            (fused, 0, 0, 2),
+            (fused, 0, 2, 4),
+            (fused, 1, 0, 2),
+            (fused, 1, 2, 4),
+            (fused, 3, 0, 1),
+            (weigh, 2, 0, 2),
+            (weigh, 3, 1, 2),
+            (weigh, 2, 2, 4),
         ):
-            step(d, v0, v1)
-            for c in range(v0 // P, v1 // P):
-                turn(turned, "turned", 4, c, terms[d][:, c * P : (c + 1) * P])
-        for c0, c1 in PIECES:
-            pick(4, c0 * P, c1 * P)
+            step(d, c0, c1)
             for c in range(c0, c1):
-                turn(plain, "plain", 1, c, picked[4][:, c * P : (c + 1) * P])
-        back = {c0: bank(n) for (c0, c1), n in zip(PIECES, (2, 3, 4))}
+                turn(("turned", c), 4 if c < 2 else 3, turned[c][:, 0:P], terms[d][:, cols(c, c + 1)])
+        weigh(3, 2, 4)
+        for c in range(blocks):
+            nc.scalar.activation(scaled[c][:], plain[:, cols(c, c + 1)], COPY, scale=column[:, c, 0:1])
+            turn_back(c, scaled[c][:])
+        for c in range(blocks):
+            nc.scalar.copy(partial[c][:], turned[c][:, 0:P])
+            turn_back(c, partial[c][:])
+        fused(5, 2, 4)
+        fused(5, 0, 2)
+        direct = keep.tile([P, HALF], F32)
+        nc.vector.tensor_tensor(direct[:], terms[3][:, cols(2, 4)], terms[5][:, cols(2, 4)], ADD)
         for c0, c1 in PIECES:
-            for c in range(c0, c1):
-                nc.scalar.activation(
-                    scaled[c][:], plain[c0][:, (c - c0) * P : (c - c0 + 1) * P], COPY, scale=column[:, c, 0:1]
-                )
-                turn(back, "back", 2, c, scaled[c][:])
-            nc.scalar.copy(partial[c0][:], turned[c0][:, 0 : (c1 - c0) * P])
-            for c in range(c0, c1):
-                turn(back, "back", 2, c, partial[c0][:, (c - c0) * P : (c - c0 + 1) * P])
-        fused(5, 0, HALF)
-        fused(5, HALF, V)
-        result = keep.tile([P, V], F32)
-        for c0, c1 in PIECES:
-            cols = slice(c0 * P, c1 * P)
-            nc.vector.tensor_tensor(result[:, cols], back[c0][:, 0 : (c1 - c0) * P], terms[5][:, cols], ADD)
-        for h in range(2):
-            nc.sync.dma_start(out=out[:, h * HALF : (h + 1) * HALF], in_=result[:, h * HALF : (h + 1) * HALF])
+            result = keep.tile([P, (c1 - c0) * P], F32, name=f"result{c0}")
+            rest = terms[5][:, cols(c0, c1)] if c0 < 2 else direct[:, cols(c0 - 2, c1 - 2)]
+            nc.vector.tensor_tensor(result[:], back[c0][:, 0 : (c1 - c0) * P], rest, ADD)
+            nc.sync.dma_start(out=out[:, cols(c0, c1)], in_=result[:])

@@ -82,19 +82,19 @@ def tile_picked_agg_lin_relu_sub_l_kernel(
             for d in range(d0, d1):
                 gates[d] = joint[:, d - d0, :]
 
-        load_list(4)
+        load_list(1)
         load_list(0)
         load_gates(0, 1)
-        load_list(1)
-        load_list(2)
         load_gates(1, 2)
         load_list(3)
-        load_gates(2, 4)
+        load_list(2)
+        load_gates(2, 3)
+        load_list(4)
+        load_gates(4, 6)
         column = keep.tile([P, V // P, 8], F32)
         with nc.allow_non_contiguous_dma(reason="one weight a partition and block"):
-            nc.sync.dma_start(out=column[:, :, 0:1], in_=gate[4, 0:1, :].rearrange("o (c p) -> p c o", p=P))
+            nc.sync.dma_start(out=column[:, :, 0:1], in_=gate[3, 0:1, :].rearrange("o (c p) -> p c o", p=P))
         load_list(5)
-        load_gates(5, 6)
 
         grouped = keep.tile([P, T, PACK], BF16, align_bytes=64)
         x_codes = keep.tile([P, T], U32, align_bytes=64)
@@ -162,8 +162,8 @@ def tile_picked_agg_lin_relu_sub_l_kernel(
         relu_on_scalar(896, 1024)
 
         blocks = V // P
-        terms = {d: keep.tile([P, V], F32, name=f"term{d}") for d in (0, 1, 2, 3, 5)}
-        picked = {d: keep.tile([P, V], F32, name=f"picked{d}") for d in (2, 3, 4)}
+        terms = {d: keep.tile([P, V], F32, name=f"term{d}") for d in (0, 1, 2, 4, 5)}
+        picked = {d: keep.tile([P, V], F32, name=f"picked{d}") for d in (1, 3, 4)}
         turned = [bank(n) for n in (4, 5, 6, 7)]
         plain = bank(0)
         back = {c0: bank(n) for (c0, c1), n in zip(PIECES, (1, 2, 3))}
@@ -199,40 +199,41 @@ def tile_picked_agg_lin_relu_sub_l_kernel(
             c0, c1 = piece_of[c]
             turn(("back", c0), 2 * (c1 - c0), back[c0][:, cols(c - c0, c - c0 + 1)], block)
 
-        for c0, c1 in PIECES:
-            pick(4, c0, c1)
+        pick(1, 0, 2)
+        pick(1, 2, 4)
+        for c0, c1 in ((0, 2), (2, 4)):
+            pick(3, c0, c1)
             for c in range(c0, c1):
-                turn("plain", blocks, plain[:, cols(c, c + 1)], picked[4][:, cols(c, c + 1)])
-        pick(2, 0, 2)
-        pick(2, 2, 4)
-        pick(3, 1, 2)
-        pick(3, 2, 4)
+                turn("plain", blocks, plain[:, cols(c, c + 1)], picked[3][:, cols(c, c + 1)])
+        for c in range(1, blocks):
+            pick(4, c, c + 1)
         for step, d, c0, c1 in (
             (fused, 0, 0, 2),
             (fused, 0, 2, 4),
-            (fused, 1, 0, 2),
-            (fused, 1, 2, 4),
-            (fused, 3, 0, 1),
-            (weigh, 2, 0, 2),
-            (weigh, 3, 1, 2),
-            (weigh, 2, 2, 4),
+            (weigh, 1, 0, 2),
+            (weigh, 1, 2, 4),
+            (fused, 2, 0, 2),
+            (fused, 2, 2, 4),
+            (fused, 4, 0, 1),
+            (weigh, 4, 1, 2),
+            (weigh, 4, 2, 3),
+            (weigh, 4, 3, 4),
         ):
             step(d, c0, c1)
             for c in range(c0, c1):
-                turn(("turned", c), 4 if c < 2 else 3, turned[c][:, 0:P], terms[d][:, cols(c, c + 1)])
-        weigh(3, 2, 4)
+                turn(("turned", c), 4, turned[c][:, 0:P], terms[d][:, cols(c, c + 1)])
         for c in range(blocks):
             nc.scalar.activation(scaled[c][:], plain[:, cols(c, c + 1)], COPY, scale=column[:, c, 0:1])
-            turn_back(c, scaled[c][:])
         for c in range(blocks):
             nc.scalar.copy(partial[c][:], turned[c][:, 0:P])
+        for c in range(blocks - 1):
+            turn_back(c, scaled[c][:])
+        for c in range(blocks):
             turn_back(c, partial[c][:])
-        fused(5, 2, 4)
+        turn_back(blocks - 1, scaled[blocks - 1][:])
         fused(5, 0, 2)
-        direct = keep.tile([P, HALF], F32)
-        nc.vector.tensor_tensor(direct[:], terms[3][:, cols(2, 4)], terms[5][:, cols(2, 4)], ADD)
+        fused(5, 2, 4)
         for c0, c1 in PIECES:
             result = keep.tile([P, (c1 - c0) * P], F32, name=f"result{c0}")
-            rest = terms[5][:, cols(c0, c1)] if c0 < 2 else direct[:, cols(c0 - 2, c1 - 2)]
-            nc.vector.tensor_tensor(result[:], back[c0][:, 0 : (c1 - c0) * P], rest, ADD)
+            nc.vector.tensor_tensor(result[:], back[c0][:, 0 : (c1 - c0) * P], terms[5][:, cols(c0, c1)], ADD)
             nc.sync.dma_start(out=out[:, cols(c0, c1)], in_=result[:])

@@ -83,6 +83,9 @@ def tile_picked_agg_lin_relu_sub_l_kernel(
                 gates[d] = joint[:, d - d0, :]
 
         load_list(1)
+        rows = keep.tile([P, P], F32)
+        nc.gpsimd.memset(rows[:], 0.0)
+        nc.sync.dma_start(out=rows[0 : V // P, :], in_=gate[3, 0:1, :].rearrange("o (c p) -> (o c) p", p=P))
         load_list(0)
         load_gates(0, 1)
         load_gates(1, 2)
@@ -91,9 +94,6 @@ def tile_picked_agg_lin_relu_sub_l_kernel(
         load_gates(2, 3)
         load_list(4)
         load_gates(4, 6)
-        column = keep.tile([P, V // P, 8], F32)
-        with nc.allow_non_contiguous_dma(reason="one weight a partition and block"):
-            nc.sync.dma_start(out=column[:, :, 0:1], in_=gate[3, 0:1, :].rearrange("o (c p) -> p c o", p=P))
         load_list(5)
 
         grouped = keep.tile([P, T, PACK], BF16, align_bytes=64)
@@ -164,11 +164,12 @@ def tile_picked_agg_lin_relu_sub_l_kernel(
         blocks = V // P
         terms = {d: keep.tile([P, V], F32, name=f"term{d}") for d in (0, 1, 2, 4, 5)}
         picked = {d: keep.tile([P, V], F32, name=f"picked{d}") for d in (1, 3, 4)}
-        turned = [bank(n) for n in (4, 5, 6, 7)]
+        turned_rows = bank(4)
+        nc.tensor.transpose(turned_rows[:, 0:P], rows[:], ident[:])
+        column = keep.tile([P, blocks], F32)
         plain = bank(0)
         back = {c0: bank(n) for (c0, c1), n in zip(PIECES, (1, 2, 3))}
         partial = [keep.tile([P, P], F32, name=f"partial{c}") for c in range(blocks)]
-        scaled = [keep.tile([P, P], F32, name=f"scaled{c}") for c in range(blocks)]
         piece_of = {c: (c0, c1) for c0, c1 in PIECES for c in range(c0, c1)}
 
         def cols(c0, c1):
@@ -201,6 +202,8 @@ def tile_picked_agg_lin_relu_sub_l_kernel(
 
         pick(1, 0, 2)
         pick(1, 2, 4)
+        nc.scalar.copy(column[:], turned_rows[:, 0:blocks])
+        turned = [bank(n) for n in (5, 6, 7, 4)]
         for c0, c1 in ((0, 2), (2, 4)):
             pick(3, c0, c1)
             for c in range(c0, c1):
@@ -222,15 +225,16 @@ def tile_picked_agg_lin_relu_sub_l_kernel(
             step(d, c0, c1)
             for c in range(c0, c1):
                 turn(("turned", c), 4, turned[c][:, 0:P], terms[d][:, cols(c, c + 1)])
+        scaled = [gates[4][:, cols(c, c + 1)] for c in range(blocks)]
         for c in range(blocks):
-            nc.scalar.activation(scaled[c][:], plain[:, cols(c, c + 1)], COPY, scale=column[:, c, 0:1])
+            nc.scalar.activation(scaled[c], plain[:, cols(c, c + 1)], COPY, scale=column[:, c : c + 1])
         for c in range(blocks):
             nc.scalar.copy(partial[c][:], turned[c][:, 0:P])
         for c in range(blocks - 1):
-            turn_back(c, scaled[c][:])
+            turn_back(c, scaled[c])
         for c in range(blocks):
             turn_back(c, partial[c][:])
-        turn_back(blocks - 1, scaled[blocks - 1][:])
+        turn_back(blocks - 1, scaled[blocks - 1])
         fused(5, 0, 2)
         fused(5, 2, 4)
         for c0, c1 in PIECES:

@@ -152,19 +152,18 @@ def tile_picked_agg_lin_relu_sub_l_kernel(
         copy_on_vector(2, 768, 896)
         copy_on_vector(2, 896, 928)
         copy_on_scalar(2, 928, 1024)
-        project(512, 640, 512)
-        project(640, 768, 512)
-        project(768, 896, 768)
-        project(896, 1024, 896)
+        for t0, t1 in ((512, 640), (640, 768), (768, 896), (896, 960), (960, 1024)):
+            project(t0, t1, t0)
         relu_on_scalar(0, 512)
-        relu_on_scalar(512, 768)
-        relu_on_vector(768, 896)
-        relu_on_scalar(896, 1024)
+        for t0 in (512, 640, 768):
+            relu_on_vector(t0, t0 + P)
+        relu_on_scalar(896, 960)
+        relu_on_scalar(960, 1024)
 
         blocks = V // P
         terms = {d: keep.tile([P, V], F32, name=f"term{d}") for d in (0, 1, 2, 4, 5)}
         picked = {d: keep.tile([P, V], F32, name=f"picked{d}") for d in (1, 3, 4)}
-        turned_rows = bank(4)
+        turned_rows = bank(6)
         nc.tensor.transpose(turned_rows[:, 0:P], rows[:], ident[:])
         column = keep.tile([P, blocks], F32)
         plain = bank(0)
@@ -203,7 +202,7 @@ def tile_picked_agg_lin_relu_sub_l_kernel(
         pick(1, 0, 2)
         pick(1, 2, 4)
         nc.scalar.copy(column[:], turned_rows[:, 0:blocks])
-        turned = [bank(n) for n in (5, 6, 7, 4)]
+        turned = [bank(n) for n in (7, 4, 5, 6)]
         for c0, c1 in ((0, 2), (2, 4)):
             pick(3, c0, c1)
             for c in range(c0, c1):

@@ -24,7 +24,7 @@ ADD = mybir.AluOpType.add
 MAX = mybir.AluOpType.max
 
 LOADS = ((0, 512), (512, 768), (768, 1024))
-PIECES = ((0, 2), (2, 3), (3, 4))
+PIECES = ((0, 1), (1, 2), (2, 3), (3, 4))
 HALF = V // 2
 
 
@@ -88,10 +88,9 @@ def tile_picked_agg_lin_relu_sub_l_kernel(
         nc.sync.dma_start(out=rows[0 : V // P, :], in_=gate[3, 0:1, :].rearrange("o (c p) -> (o c) p", p=P))
         load_list(0)
         load_gates(0, 1)
-        load_gates(1, 2)
+        load_gates(1, 3)
         load_list(3)
         load_list(2)
-        load_gates(2, 3)
         load_list(4)
         load_gates(4, 6)
         load_list(5)
@@ -167,7 +166,6 @@ def tile_picked_agg_lin_relu_sub_l_kernel(
         nc.tensor.transpose(turned_rows[:, 0:P], rows[:], ident[:])
         column = keep.tile([P, blocks], F32)
         plain = bank(0)
-        back = {c0: bank(n) for (c0, c1), n in zip(PIECES, (1, 2, 3))}
         partial = [keep.tile([P, P], F32, name=f"partial{c}") for c in range(blocks)]
         piece_of = {c: (c0, c1) for c0, c1 in PIECES for c in range(c0, c1)}
 
@@ -229,6 +227,7 @@ def tile_picked_agg_lin_relu_sub_l_kernel(
             nc.scalar.activation(scaled[c], plain[:, cols(c, c + 1)], COPY, scale=column[:, c : c + 1])
         for c in range(blocks):
             nc.scalar.copy(partial[c][:], turned[c][:, 0:P])
+        back = {c0: bank(n) for (c0, c1), n in zip(PIECES, (1, 2, 3, 7))}
         for c in range(blocks - 1):
             turn_back(c, scaled[c])
         for c in range(blocks):

@@ -142,16 +142,19 @@ def tile_picked_agg_lin_relu_sub_l_kernel(
         copy_on_vector(0, 0, 672)
         copy_on_scalar(0, 672, 1024)
         copy_on_vector(2, 0, 256)
-        copy_on_vector(2, 256, 384)
-        copy_on_scalar(2, 384, 512)
+        copy_on_vector(2, 256, 320)
+        copy_on_scalar(2, 320, 512)
         project(0, 256, 0)
         project(256, 512, 0)
         copy_on_scalar(2, 512, 640)
-        copy_on_scalar(2, 640, 768)
+        copy_on_scalar(2, 640, 704)
+        copy_on_vector(2, 704, 768)
+        project(512, 640, 512)
+        project(640, 768, 640)
+        copy_on_scalar(2, 896, 960)
+        copy_on_scalar(2, 960, 1024)
         copy_on_vector(2, 768, 896)
-        copy_on_vector(2, 896, 928)
-        copy_on_scalar(2, 928, 1024)
-        for t0, t1 in ((512, 640), (640, 768), (768, 896), (896, 960), (960, 1024)):
+        for t0, t1 in ((896, 960), (768, 896), (960, 1024)):
             project(t0, t1, t0)
         relu_on_scalar(0, 512)
         for t0 in (512, 640, 768):

from contextlib import ExitStack

import concourse.mybir as mybir
from concourse.masks import make_identity

K, T, D, V, N = 512, 1024, 6, 512, 128
P = 128
PACK = 4
BANK = 512
LINE = 4
FLOPS = 2 * K * N * T + 2 * D * N * V

F32 = mybir.dt.float32
BF16 = mybir.dt.bfloat16
I32 = mybir.dt.int32
U32 = mybir.dt.uint32
U16 = mybir.dt.uint16
U8 = mybir.dt.uint8
FP8X4 = mybir.dt.float8_e4m3fn_x4
RELU = mybir.ActivationFunctionType.Relu
COPY = mybir.ActivationFunctionType.Copy
MULT = mybir.AluOpType.mult
ADD = mybir.AluOpType.add
MAX = mybir.AluOpType.max

LOADS = ((0, 512), (512, 768), (768, 1024))
PIECES = ((0, 1), (1, 2), (2, 3), (3, 4))
HALF = V // 2


def tile_picked_agg_lin_relu_sub_l_kernel(
    tc, xT, w_words, w_scales, b, gate, pos1, pos2, pos3, pos4, pos5, pos6, out
):
    nc = tc.nc
    with ExitStack() as ctx:
        lists = ctx.enter_context(tc.tile_pool(name="lists", bufs=1))
        keep = ctx.enter_context(tc.tile_pool(name="keep", bufs=1))
        psum = ctx.enter_context(tc.psum_pool(name="psum", bufs=1))

        def bank(n):
            return psum.tile([P, BANK], F32, name=f"bank{n}")

        offsets = [lists.tile([P, V // 16], U16, name=f"offsets{d}") for d in range(D)]

        ident = keep.tile([P, P], F32)
        make_identity(nc, ident[:])

        w_scale = keep.tile([P, N], U8, align_bytes=64)
        nc.vector.memset(w_scale[:].bitcast(I32), 0)

        w_codes = keep.tile([P, N * PACK], U8, align_bytes=64)
        nc.scalar.dma_start(out=w_codes[:].bitcast(I32), in_=w_words.rearrange("a p m r -> (a p) (m r)").bitcast(I32))
        bias = keep.tile([P, 1], F32)

        x_rows = xT.rearrange("(p j) t -> p j t", j=PACK)
        raws = {}

        def load_x(j0, t0, t1):
            raws[j0, t0, t1] = keep.tile([P, 2, t1 - t0], F32, name=f"raw{len(raws)}")
            nc.sync.dma_start(out=raws[j0, t0, t1][:], in_=x_rows[:, j0 : j0 + 2, t0:t1])

        load_x(0, 0, T)
        scale_rows = w_scales.rearrange("a q m -> (a q) m")
        for quadrant in range(4):
            nc.sync.dma_start(
                out=w_scale[32 * quadrant : 32 * quadrant + 4, :].bitcast(I32),
                in_=scale_rows[4 * quadrant : 4 * quadrant + 4, :].bitcast(I32),
            )
        for t0, t1 in LOADS:
            load_x(2, t0, t1)
        nc.sync.dma_start(out=bias[:], in_=b)

        positions = (pos1, pos2, pos3, pos4, pos5, pos6)
        gates = {}

        def load_list(d):
            nc.sync.dma_start(out=offsets[d][:], in_=positions[d])

        def load_gates(d0, d1):
            joint = keep.tile([P, d1 - d0, V], F32, name=f"gates{d0}")
            nc.sync.dma_start(out=joint[:], in_=gate[d0:d1].rearrange("d m v -> m d v"))
            for d in range(d0, d1):
                gates[d] = joint[:, d - d0, :]

        load_list(1)
        rows = keep.tile([P, P], F32)
        nc.gpsimd.memset(rows[:], 0.0)
        nc.sync.dma_start(out=rows[0 : V // P, :], in_=gate[3, 0:1, :].rearrange("o (c p) -> (o c) p", p=P))
        load_list(0)
        load_gates(0, 1)
        load_gates(1, 3)
        load_list(3)
        load_list(2)
        load_list(4)
        load_gates(4, 6)
        load_list(5)

        grouped = keep.tile([P, T, PACK], BF16, align_bytes=64)
        x_codes = keep.tile([P, T], U32, align_bytes=64)
        x_scale = keep.tile([P, T], U8, align_bytes=64)
        y = keep.tile([P, T], F32)
        products = {}

        def loaded(j0, t0, t1):
            for (j, l0, l1), raw in raws.items():
                if j == j0 and l0 <= t0 and t1 <= l1:
                    return raw[:, :, t0 - l0 : t1 - l0].rearrange("p j (c i) -> p c j i", i=LINE)

        def laid(j0, t0, t1):
            return grouped[:, t0:t1, j0 : j0 + 2].rearrange("p (c i) j -> p c j i", i=LINE)

        def copy_on_vector(j0, t0, t1):
            nc.vector.tensor_copy(laid(j0, t0, t1), loaded(j0, t0, t1))

        def copy_on_scalar(j0, t0, t1):
            nc.scalar.copy(laid(j0, t0, t1), loaded(j0, t0, t1))

        def project(t0, t1, first):
            nc.vector.quantize_mx(
                out=x_codes[:, t0:t1].bitcast(FP8X4),
                scales=x_scale[:, t0:t1],
                in_=grouped[:, t0:t1, :].rearrange("p t j -> p (t j)"),
            )
            if first not in products:
                products[first] = bank(len(products))
            nc.tensor.matmul_mx(
                out=products[first][:, t0 - first : t1 - first],
                lhsT=w_codes[:].bitcast(FP8X4),
                lhsT_scale=w_scale[:],
                rhs=x_codes[:, t0:t1].bitcast(FP8X4),
                rhs_scale=x_scale[:, t0:t1],
                start=True,
                stop=True,
            )

        def relu_on_scalar(t0, t1):
            nc.scalar.activation(y[:, t0:t1], products[t0][:, 0 : t1 - t0], RELU, bias=bias[:])

        def relu_on_vector(t0, t1):
            nc.vector.tensor_scalar(y[:, t0:t1], products[t0][:, 0 : t1 - t0], bias[:], 0.0, ADD, MAX)

        copy_on_vector(0, 0, 672)
        copy_on_scalar(0, 672, 1024)
        copy_on_vector(2, 0, 256)
        copy_on_vector(2, 256, 320)
        copy_on_scalar(2, 320, 512)
        project(0, 256, 0)
        project(256, 512, 0)
        copy_on_scalar(2, 512, 640)
        copy_on_scalar(2, 640, 704)
        copy_on_vector(2, 704, 768)
        project(512, 640, 512)
        project(640, 768, 640)
        copy_on_scalar(2, 896, 960)
        copy_on_scalar(2, 960, 1024)
        copy_on_vector(2, 768, 896)
        for t0, t1 in ((896, 960), (768, 896), (960, 1024)):
            project(t0, t1, t0)
        relu_on_scalar(0, 512)
        for t0 in (512, 640, 768):
            relu_on_vector(t0, t0 + P)
        relu_on_scalar(896, 960)
        relu_on_scalar(960, 1024)

        blocks = V // P
        terms = {d: keep.tile([P, V], F32, name=f"term{d}") for d in (0, 1, 2, 4, 5)}
        picked = {d: keep.tile([P, V], F32, name=f"picked{d}") for d in (1, 3, 4)}
        turned_rows = bank(6)
        nc.tensor.transpose(turned_rows[:, 0:P], rows[:], ident[:])
        column = keep.tile([P, blocks], F32)
        plain = bank(0)
        partial = [keep.tile([P, P], F32, name=f"partial{c}") for c in range(blocks)]
        piece_of = {c: (c0, c1) for c0, c1 in PIECES for c in range(c0, c1)}

        def cols(c0, c1):
            return slice(c0 * P, c1 * P)

        def entries(d, c0, c1):
            return y[:].indirect(offsets[d][:, c0 * P // 16 : c1 * P // 16])

        def fused(d, c0, c1):
            nc.vector.tensor_tensor(terms[d][:, cols(c0, c1)], entries(d, c0, c1), gates[d][:, cols(c0, c1)], MULT)

        def pick(d, c0, c1):
            nc.scalar.activation(picked[d][:, cols(c0, c1)], entries(d, c0, c1), COPY)

        def weigh(d, c0, c1):
            nc.vector.tensor_tensor(terms[d][:, cols(c0, c1)], picked[d][:, cols(c0, c1)], gates[d][:, cols(c0, c1)], MULT)

        passes = {}

        def turn(name, count, target, block):
            done = passes.get(name, 0)
            nc.tensor.matmul(
                target, lhsT=block, rhs=ident[:], is_transpose=True, start=(done == 0), stop=(done == count - 1)
            )
            passes[name] = done + 1

        def turn_back(c, block):
            c0, c1 = piece_of[c]
            turn(("back", c0), 2 * (c1 - c0), back[c0][:, cols(c - c0, c - c0 + 1)], block)

        pick(1, 0, 2)
        pick(1, 2, 4)
        nc.scalar.copy(column[:], turned_rows[:, 0:blocks])
        turned = [bank(n) for n in (7, 4, 5, 6)]
        for c0, c1 in ((0, 2), (2, 4)):
            pick(3, c0, c1)
            for c in range(c0, c1):
                turn("plain", blocks, plain[:, cols(c, c + 1)], picked[3][:, cols(c, c + 1)])
        for c in range(1, blocks):
            pick(4, c, c + 1)
        for step, d, c0, c1 in (
            (fused, 0, 0, 2),
            (fused, 0, 2, 4),
            (weigh, 1, 0, 2),
            (weigh, 1, 2, 4),
            (fused, 2, 0, 2),
            (fused, 2, 2, 4),
            (fused, 4, 0, 1),
            (weigh, 4, 1, 2),
            (weigh, 4, 2, 3),
            (weigh, 4, 3, 4),
        ):
            step(d, c0, c1)
            for c in range(c0, c1):
                turn(("turned", c), 4, turned[c][:, 0:P], terms[d][:, cols(c, c + 1)])
        scaled = [gates[4][:, cols(c, c + 1)] for c in range(blocks)]
        for c in range(blocks):
            nc.scalar.activation(scaled[c], plain[:, cols(c, c + 1)], COPY, scale=column[:, c : c + 1])
        for c in range(blocks):
            nc.scalar.copy(partial[c][:], turned[c][:, 0:P])
        back = {c0: bank(n) for (c0, c1), n in zip(PIECES, (1, 2, 3, 7))}
        for c in range(blocks - 1):
            turn_back(c, scaled[c])
        for c in range(blocks):
            turn_back(c, partial[c][:])
        turn_back(blocks - 1, scaled[blocks - 1])
        fused(5, 0, 2)
        fused(5, 2, 4)
        for c0, c1 in PIECES:
            result = keep.tile([P, (c1 - c0) * P], F32, name=f"result{c0}")
            nc.vector.tensor_tensor(result[:], back[c0][:, 0 : (c1 - c0) * P], terms[5][:, cols(c0, c1)], ADD)
            nc.sync.dma_start(out=out[:, cols(c0, c1)], in_=result[:])
